import numpy as np
import ml_dtypes


def mxq(x, axis, fmt="e4m3"):
    dtype, down = {"e4m3": (ml_dtypes.float8_e4m3fn, 7), "e5m2": (ml_dtypes.float8_e5m2, 14)}[fmt]
    v = np.moveaxis(np.asarray(x, np.float32).astype(ml_dtypes.bfloat16).astype(np.float64), axis, -1)
    blocks = v.reshape(v.shape[:-1] + (-1, 32))
    amax = np.abs(blocks).max(-1, keepdims=True)
    byte = np.maximum(np.where(amax > 0, np.frexp(amax)[1] - 1 + 127, 0) - down, 1)
    scale = np.exp2(byte - 127.0)
    codes = (blocks / scale).astype(np.float32).astype(dtype).astype(np.float64)
    return np.moveaxis((codes * scale).reshape(v.shape), -1, axis)


WIDE = False


def mx_kscale(k):
    if not WIDE:
        return np.ones(k)
    levels = np.array([10, -10, 5, -5, 0])
    if k % 512:
        return np.exp2(np.random.permutation(np.resize(levels, k // 32))).repeat(32)
    a = np.empty((k // 512, 16))
    for p in range(k // 512):
        a[p, :8] = np.random.permutation(np.resize(levels, 8))
        for g in range(8):
            far = levels[np.abs(levels - a[p, g]) >= 10]
            a[p, g + 8] = far[np.random.randint(len(far))]
    return np.exp2(a.ravel()).repeat(32)


def f64(x):
    return np.asarray(x).astype(np.float64)


def striped(idx):
    return np.tile(idx.reshape(-1, 16).T, (8, 1)).astype(np.uint16)


def unstriped(offs):
    return offs[:16].T.reshape(-1).astype(np.int64)


def pack_weight(w):
    k, n = w.shape
    w = f64(np.asarray(w, np.float32).astype(ml_dtypes.bfloat16)).reshape(k // 32, 32, n)
    amax = np.abs(w).max(1)
    byte = np.clip(np.where(amax > 0, np.frexp(amax)[1] - 1 + 127 - 7, 1), 1, 254)
    scaled = (w * np.exp2(127.0 - byte)[:, None, :]).reshape(k, n).astype(np.float32)
    words = np.ascontiguousarray(scaled.reshape(k // 512, 128, 4, n).transpose(0, 1, 3, 2)).astype(ml_dtypes.float8_e4m3fn).view(np.uint8)
    return words, np.ascontiguousarray(byte.astype(np.uint8).reshape(k // 512, 16, n))


def unpack_weight(words, scales):
    g, p, n, _ = words.shape
    vals = np.ascontiguousarray(words).view(ml_dtypes.float8_e4m3fn).astype(np.float64) * np.repeat(np.exp2(scales.astype(np.float64) - 127.0), 8, axis=1)[..., None]
    return vals.transpose(0, 1, 3, 2).reshape(g * 512, n)


K, T, S, V, H, N = 512, 1024, 512, 256, 512, 128


def setup_inputs():
    n = np.random.standard_normal
    s = mx_kscale(K)[:, None]
    u = mx_kscale(H)
    near = np.random.permutation(S)
    packed_xT = pack_weight(n((K, T)) * s)
    return {
        "x_words": packed_xT[0],
        "x_scales": packed_xT[1],
        "w1": (n((K, H)) / np.sqrt(K) / s).astype(np.float32),
        "w2": (n((H, N)) / np.sqrt(H) / u[:, None]).astype(np.float32),
        "damp": (np.random.uniform(0.5, 1.0, (H, 1)) * u[:, None]).astype(np.float32),
        "offs": striped(np.random.permutation(T)[:S]),
        "pos1": striped(near[:V]),
        "pos2": striped(near[V:]),
        "pos3": striped(np.random.permutation(S)[:V]),
    }


def reference(x_words, x_scales, w1, w2, damp, offs, pos1, pos2, pos3):
    xq = unpack_weight(x_words, x_scales)[:, unstriped(offs)]
    h = np.tanh(0.5 * ((mxq(f64(w1), 0, "e4m3").T @ xq)))
    z = (h[:, unstriped(pos1)] * h[:, unstriped(pos2)]) * h[:, unstriped(pos3)]
    rr = f64(damp) * (np.log(0.98 * z + 1.0) - np.log(-0.98 * z + 1.0))
    return mxq(f64(w2), 0, "e4m3").T @ mxq(rr, 0, "e4m3")

@@ -1,0 +1,163 @@
+from contextlib import ExitStack
+
+import concourse.mybir as mybir
+
+K, T, S, V, H, N = 512, 1024, 512, 256, 512, 128
+FLOPS = 2 * K * H * S + 2 * H * N * V
+
+F32 = mybir.dt.float32
+BF16 = mybir.dt.bfloat16
+I32 = mybir.dt.int32
+U32 = mybir.dt.uint32
+U16 = mybir.dt.uint16
+U8 = mybir.dt.uint8
+FP8X4 = mybir.dt.float8_e4m3fn_x4
+ACT = mybir.ActivationFunctionType
+ALU = mybir.AluOpType
+
+P = 128
+PACK = 4
+GROUP = 8
+RUN = 4
+HALF = V // 2
+
+
+def tile_picked_yldpc_bp_p_kernel(tc, x_words, x_scales, w1, w2, damp, offs, pos1, pos2, pos3, out):
+    nc = tc.nc
+    with ExitStack() as ctx:
+        keep = ctx.enter_context(tc.tile_pool(name="keep", bufs=1))
+        psum = ctx.enter_context(tc.psum_pool(name="psum", bufs=1))
+
+        offs_t = keep.tile([P, S // 16], U16, name="offs_t")
+        pos_t = [keep.tile([P, V // 16], U16, name="pos_t%d" % d) for d in range(3)]
+        xw = keep.tile([P, T], U32, name="xw", align_bytes=64)
+        xs = keep.tile([P, T], U8, name="xs", align_bytes=64)
+        w1_raw = keep.tile([P, PACK, H], F32, name="w1_raw", align_bytes=64)
+        w2_raw = keep.tile([P, PACK, N], F32, name="w2_raw", align_bytes=64)
+        damp_pad = keep.tile([P, PACK, 8], F32, name="damp_pad", align_bytes=64)
+        warm = keep.tile([P, 8], F32, name="warm", align_bytes=64)
+        warm_out = keep.tile([P, 8], F32, name="warm_out", align_bytes=64)
+
+        nc.vector.memset(warm[:], 0.0)
+        nc.sync.dma_start(xw[:].bitcast(I32), x_words[0].rearrange("p n t -> p (n t)").bitcast(I32))
+        nc.sync.dma_start(offs_t[:], offs)
+        for q in range(4):
+            nc.sync.dma_start(xs[32 * q : 32 * q + 32, :].bitcast(I32),
+                                x_scales[0, 4 * q : 4 * q + 4, :].bitcast(I32).unsqueeze(0).to_broadcast([8, 4, T // 4]))
+        nc.sync.dma_start(w1_raw[:], w1.rearrange("(p j) c -> p j c", j=PACK))
+        nc.scalar.activation(warm_out[:], warm[:], ACT.Tanh, scale=0.5)
+        w2_rows = w2.rearrange("(b t r) n -> t b r n", t=PACK, r=GROUP)
+        for t in range(PACK):
+            nc.sync.dma_start(w2_raw[:, t, :], w2_rows[t])
+        nc.sync.dma_start(pos_t[0][:], pos1)
+        nc.sync.dma_start(pos_t[1][:], pos2)
+        nc.sync.dma_start(pos_t[2][:], pos3)
+        damp_rows = damp.rearrange("(b t r) o -> t b r o", t=PACK, r=GROUP)
+        for t in range(PACK):
+            nc.sync.dma_start(damp_pad[:, t, 0:1], damp_rows[t])
+
+        xg_s = keep.tile([P, S], U8, name="xg_s", align_bytes=64)
+        xg_w = keep.tile([P, S], U32, name="xg_w", align_bytes=64)
+        nc.vector.tensor_copy(xg_s[:], xs[:].indirect(offs_t[:]))
+        nc.vector.tensor_copy(xg_w[:], xw[:].indirect(offs_t[:]))
+
+        w1_cols = w1_raw[:].rearrange("p j (b t u i) -> p t b u j i", t=PACK, u=GROUP // RUN, i=RUN)
+        w1_bf = [keep.tile([P, P * PACK], BF16, name="w1_bf%d" % t, align_bytes=64) for t in range(PACK)]
+        w1_c = [keep.tile([P, P], U32, name="w1_c%d" % t, align_bytes=64) for t in range(PACK)]
+        w1_s = [keep.tile([P, P], U8, name="w1_s%d" % t, align_bytes=64) for t in range(PACK)]
+        h = [keep.tile([P, S], F32, name="h%d" % t, align_bytes=64) for t in range(PACK)]
+
+        def cast_w1(t):
+            dst = w1_bf[t][:].rearrange("p (b u i j) -> p b u j i", u=GROUP // RUN, i=RUN, j=PACK)
+            if t == 0:
+                nc.vector.tensor_copy(dst, w1_cols[:, t])
+            else:
+                nc.scalar.copy(dst, w1_cols[:, t])
+
+        def first_product(t, cols, name):
+            pre = psum.tile([P, cols.stop - cols.start], F32, name=name)
+            nc.tensor.matmul_mx(out=pre[:], lhsT=w1_c[t][:].bitcast(FP8X4), lhsT_scale=w1_s[t][:],
+                                rhs=xg_w[:, cols].bitcast(FP8X4), rhs_scale=xg_s[:, cols], start=True, stop=True)
+            return pre
+
+        for t in range(PACK):
+            cast_w1(t)
+        for t in range(PACK):
+            nc.vector.quantize_mx(out=w1_c[t][:].bitcast(FP8X4), scales=w1_s[t][:], in_=w1_bf[t][:])
+        parts = [(0, slice(0, S // 2)), (0, slice(S // 2, S))] + [(t, slice(0, S)) for t in range(1, PACK)]
+        pres = [first_product(t, cols, "pre%d" % k) for k, (t, cols) in enumerate(parts)]
+        for pre, (t, cols) in zip(pres, parts):
+            nc.scalar.activation(h[t][:, cols], pre[:], ACT.Tanh, scale=0.5)
+
+        w2_bf = w1_bf[PACK - 1]
+        w2_c = keep.tile([P, N], U32, name="w2_c", align_bytes=64)
+        w2_s = keep.tile([P, N], U8, name="w2_s", align_bytes=64)
+        nc.vector.tensor_copy(w2_bf[:].rearrange("p (c i t) -> p c t i", i=RUN, t=PACK),
+                              w2_raw[:].rearrange("p t (c i) -> p c t i", i=RUN))
+        nc.vector.quantize_mx(out=w2_c[:].bitcast(FP8X4), scales=w2_s[:], in_=w2_bf[:])
+
+        items = [(t, 0, V) for t in range(PACK - 1)] + [(PACK - 1, 0, HALF), (PACK - 1, HALF, V)]
+        last = len(items) - 1
+        g1 = [keep.tile([P, b - a], F32, name="g1_%d" % k, align_bytes=64) for k, (t, a, b) in enumerate(items)]
+        g2 = [keep.tile([P, b - a], F32, name="g2_%d" % k, align_bytes=64) for k, (t, a, b) in enumerate(items)]
+        z = [keep.tile([P, b - a], F32, name="z%d" % k, align_bytes=64) for k, (t, a, b) in enumerate(items)]
+        lp = [keep.tile([P, b - a], F32, name="lp%d" % k, align_bytes=64) for k, (t, a, b) in enumerate(items)]
+        lm = [keep.tile([P, b - a], F32, name="lm%d" % k, align_bytes=64) for k, (t, a, b) in enumerate(items)]
+        lmd = [keep.tile([P, b - a], F32, name="lmd%d" % k, align_bytes=64) for k, (t, a, b) in enumerate(items)]
+        rr = keep.tile([P, PACK, V], BF16, name="rr", align_bytes=64)
+
+        def picked(d, k):
+            t, a, b = items[k]
+            return h[t][:].indirect(pos_t[d][:, a // 16 : b // 16])
+
+        def gather(d, k):
+            if d == 0:
+                nc.vector.tensor_copy(g1[k][:], picked(0, k))
+            elif d == 1:
+                nc.vector.tensor_tensor(g2[k][:], picked(1, k), g1[k][:], ALU.mult)
+            else:
+                nc.vector.tensor_tensor(z[k][:], picked(2, k), g2[k][:], ALU.mult)
+
+        def logs(k):
+            t = items[k][0]
+            nc.scalar.activation(lm[k][:], z[k][:], ACT.Ln, scale=-0.98, bias=1.0)
+            nc.scalar.activation(lp[k][:], z[k][:], ACT.Ln, scale=0.98, bias=1.0)
+            nc.scalar.activation(lmd[k][:], lm[k][:], ACT.Copy, scale=damp_pad[:, t, 0:1])
+
+        def damped(k):
+            t, a, b = items[k]
+            nc.vector.scalar_tensor_tensor(rr[:, t, a:b], lp[k][:], damp_pad[:, t, 0:1], lmd[k][:], ALU.mult, ALU.subtract)
+
+        for step in range(len(items) + 2):
+            for d in range(3):
+                k = step - d
+                if 0 <= k <= last:
+                    gather(d, k)
+                    if d == 2:
+                        logs(k)
+            if 0 <= step - 3 < last - 1:
+                damped(step - 3)
+
+        woven = [keep.tile([P, HALF * PACK], BF16, name="woven%d" % c, align_bytes=64) for c in range(2)]
+        rr_c = [keep.tile([P, HALF], U32, name="rr_c%d" % c, align_bytes=64) for c in range(2)]
+        rr_s = [keep.tile([P, HALF], U8, name="rr_s%d" % c, align_bytes=64) for c in range(2)]
+        res = [keep.tile([P, HALF], F32, name="res%d" % c, align_bytes=64) for c in range(2)]
+
+        def weave(c):
+            nc.vector.tensor_copy(woven[c][:].rearrange("p (c i t) -> p c t i", i=RUN, t=PACK),
+                                  rr[:, :, c * HALF : (c + 1) * HALF].rearrange("p t (c i) -> p c t i", i=RUN))
+
+        def second_product(c):
+            acc = psum.tile([P, HALF], F32, name="acc%d" % c)
+            nc.vector.quantize_mx(out=rr_c[c][:].bitcast(FP8X4), scales=rr_s[c][:], in_=woven[c][:])
+            nc.tensor.matmul_mx(out=acc[:], lhsT=w2_c[:].bitcast(FP8X4), lhsT_scale=w2_s[:],
+                                rhs=rr_c[c][:].bitcast(FP8X4), rhs_scale=rr_s[c][:], start=True, stop=True)
+            nc.scalar.copy(res[c][:], acc[:])
+            nc.sync.dma_start(out[:, c * HALF : (c + 1) * HALF], res[c][:])
+
+        damped(last - 1)
+        weave(0)
+        damped(last)
+        second_product(0)
+        weave(1)
+        second_product(1)

@@ -38,20 +38,20 @@ def tile_picked_yldpc_bp_p_kernel(tc, x_words, x_scales, w1, w2, damp, offs, pos
         warm = keep.tile([P, 8], F32, name="warm", align_bytes=64)
         warm_out = keep.tile([P, 8], F32, name="warm_out", align_bytes=64)
 
+        nc.vector.memset(xs[:].bitcast(I32), 0)
         nc.vector.memset(warm[:], 0.0)
         nc.sync.dma_start(xw[:].bitcast(I32), x_words[0].rearrange("p n t -> p (n t)").bitcast(I32))
         nc.sync.dma_start(offs_t[:], offs)
+        nc.sync.dma_start(pos_t[0][:], pos1)
         for q in range(4):
-            nc.sync.dma_start(xs[32 * q : 32 * q + 32, :].bitcast(I32),
-                                x_scales[0, 4 * q : 4 * q + 4, :].bitcast(I32).unsqueeze(0).to_broadcast([8, 4, T // 4]))
+            nc.sync.dma_start(xs[32 * q : 32 * q + 4, :].bitcast(I32), x_scales[0, 4 * q : 4 * q + 4, :].bitcast(I32))
         nc.sync.dma_start(w1_raw[:], w1.rearrange("(p j) c -> p j c", j=PACK))
         nc.scalar.activation(warm_out[:], warm[:], ACT.Tanh, scale=0.5)
+        nc.sync.dma_start(pos_t[1][:], pos2)
+        nc.sync.dma_start(pos_t[2][:], pos3)
         w2_rows = w2.rearrange("(b t r) n -> t b r n", t=PACK, r=GROUP)
         for t in range(PACK):
             nc.sync.dma_start(w2_raw[:, t, :], w2_rows[t])
-        nc.sync.dma_start(pos_t[0][:], pos1)
-        nc.sync.dma_start(pos_t[1][:], pos2)
-        nc.sync.dma_start(pos_t[2][:], pos3)
         damp_rows = damp.rearrange("(b t r) o -> t b r o", t=PACK, r=GROUP)
         for t in range(PACK):
             nc.sync.dma_start(damp_pad[:, t, 0:1], damp_rows[t])
@@ -62,14 +62,15 @@ def tile_picked_yldpc_bp_p_kernel(tc, x_words, x_scales, w1, w2, damp, offs, pos
         nc.vector.tensor_copy(xg_w[:], xw[:].indirect(offs_t[:]))
 
         w1_cols = w1_raw[:].rearrange("p j (b t u i) -> p t b u j i", t=PACK, u=GROUP // RUN, i=RUN)
-        w1_bf = [keep.tile([P, P * PACK], BF16, name="w1_bf%d" % t, align_bytes=64) for t in range(PACK)]
+        w1_bf = [keep.tile([P, P * PACK], BF16, name="w1_bf%d" % t, align_bytes=64) for t in range(PACK - 1)]
+        w1_bf.append(w1_bf[0])
         w1_c = [keep.tile([P, P], U32, name="w1_c%d" % t, align_bytes=64) for t in range(PACK)]
         w1_s = [keep.tile([P, P], U8, name="w1_s%d" % t, align_bytes=64) for t in range(PACK)]
         h = [keep.tile([P, S], F32, name="h%d" % t, align_bytes=64) for t in range(PACK)]
 
         def cast_w1(t):
             dst = w1_bf[t][:].rearrange("p (b u i j) -> p b u j i", u=GROUP // RUN, i=RUN, j=PACK)
-            if t == 0:
+            if t in (0, PACK - 1):
                 nc.vector.tensor_copy(dst, w1_cols[:, t])
             else:
                 nc.scalar.copy(dst, w1_cols[:, t])
@@ -80,63 +81,54 @@ def tile_picked_yldpc_bp_p_kernel(tc, x_words, x_scales, w1, w2, damp, offs, pos
                                 rhs=xg_w[:, cols].bitcast(FP8X4), rhs_scale=xg_s[:, cols], start=True, stop=True)
             return pre
 
-        for t in range(PACK):
+        for t in range(PACK - 1):
             cast_w1(t)
         for t in range(PACK):
+            if t == 1:
+                cast_w1(PACK - 1)
             nc.vector.quantize_mx(out=w1_c[t][:].bitcast(FP8X4), scales=w1_s[t][:], in_=w1_bf[t][:])
         parts = [(0, slice(0, S // 2)), (0, slice(S // 2, S))] + [(t, slice(0, S)) for t in range(1, PACK)]
         pres = [first_product(t, cols, "pre%d" % k) for k, (t, cols) in enumerate(parts)]
         for pre, (t, cols) in zip(pres, parts):
             nc.scalar.activation(h[t][:, cols], pre[:], ACT.Tanh, scale=0.5)
 
-        w2_bf = w1_bf[PACK - 1]
+        w2_bf = w1_bf[PACK - 2]
         w2_c = keep.tile([P, N], U32, name="w2_c", align_bytes=64)
         w2_s = keep.tile([P, N], U8, name="w2_s", align_bytes=64)
-        nc.vector.tensor_copy(w2_bf[:].rearrange("p (c i t) -> p c t i", i=RUN, t=PACK),
+        nc.scalar.copy(w2_bf[:].rearrange("p (c i t) -> p c t i", i=RUN, t=PACK),
                               w2_raw[:].rearrange("p t (c i) -> p c t i", i=RUN))
-        nc.vector.quantize_mx(out=w2_c[:].bitcast(FP8X4), scales=w2_s[:], in_=w2_bf[:])
 
-        items = [(t, 0, V) for t in range(PACK - 1)] + [(PACK - 1, 0, HALF), (PACK - 1, HALF, V)]
-        last = len(items) - 1
-        g1 = [keep.tile([P, b - a], F32, name="g1_%d" % k, align_bytes=64) for k, (t, a, b) in enumerate(items)]
-        g2 = [keep.tile([P, b - a], F32, name="g2_%d" % k, align_bytes=64) for k, (t, a, b) in enumerate(items)]
-        z = [keep.tile([P, b - a], F32, name="z%d" % k, align_bytes=64) for k, (t, a, b) in enumerate(items)]
-        lp = [keep.tile([P, b - a], F32, name="lp%d" % k, align_bytes=64) for k, (t, a, b) in enumerate(items)]
-        lm = [keep.tile([P, b - a], F32, name="lm%d" % k, align_bytes=64) for k, (t, a, b) in enumerate(items)]
-        lmd = [keep.tile([P, b - a], F32, name="lmd%d" % k, align_bytes=64) for k, (t, a, b) in enumerate(items)]
+        halves = [slice(c * HALF, (c + 1) * HALF) for c in range(2)]
+        g1 = [keep.tile([P, V], F32, name="g1_%d" % t, align_bytes=64) for t in range(PACK)]
+        g2 = [keep.tile([P, V], F32, name="g2_%d" % t, align_bytes=64) for t in range(PACK)]
+        z = [keep.tile([P, V], F32, name="z%d" % t, align_bytes=64) for t in range(PACK)]
+        lp = [keep.tile([P, V], F32, name="lp%d" % t, align_bytes=64) for t in range(PACK)]
+        lm = [keep.tile([P, V], F32, name="lm%d" % t, align_bytes=64) for t in range(PACK)]
+        lmd = [keep.tile([P, V], F32, name="lmd%d" % t, align_bytes=64) for t in range(PACK)]
         rr = keep.tile([P, PACK, V], BF16, name="rr", align_bytes=64)
 
-        def picked(d, k):
-            t, a, b = items[k]
-            return h[t][:].indirect(pos_t[d][:, a // 16 : b // 16])
+        def picked(d, t, cols):
+            return h[t][:].indirect(pos_t[d][:, cols.start // 16 : cols.stop // 16])
 
-        def gather(d, k):
-            if d == 0:
-                nc.vector.tensor_copy(g1[k][:], picked(0, k))
-            elif d == 1:
-                nc.vector.tensor_tensor(g2[k][:], picked(1, k), g1[k][:], ALU.mult)
-            else:
-                nc.vector.tensor_tensor(z[k][:], picked(2, k), g2[k][:], ALU.mult)
+        def logs(t, cols):
+            nc.scalar.activation(lm[t][:, cols], z[t][:, cols], ACT.Ln, scale=-0.98, bias=1.0)
+            nc.scalar.activation(lp[t][:, cols], z[t][:, cols], ACT.Ln, scale=0.98, bias=1.0)
+            nc.scalar.activation(lmd[t][:, cols], lm[t][:, cols], ACT.Copy, scale=damp_pad[:, t, 0:1])
 
-        def logs(k):
-            t = items[k][0]
-            nc.scalar.activation(lm[k][:], z[k][:], ACT.Ln, scale=-0.98, bias=1.0)
-            nc.scalar.activation(lp[k][:], z[k][:], ACT.Ln, scale=0.98, bias=1.0)
-            nc.scalar.activation(lmd[k][:], lm[k][:], ACT.Copy, scale=damp_pad[:, t, 0:1])
+        def damped(t, cols):
+            nc.vector.scalar_tensor_tensor(rr[:, t, cols], lp[t][:, cols], damp_pad[:, t, 0:1], lmd[t][:, cols], ALU.mult, ALU.subtract)
 
-        def damped(k):
-            t, a, b = items[k]
-            nc.vector.scalar_tensor_tensor(rr[:, t, a:b], lp[k][:], damp_pad[:, t, 0:1], lmd[k][:], ALU.mult, ALU.subtract)
-
-        for step in range(len(items) + 2):
-            for d in range(3):
-                k = step - d
-                if 0 <= k <= last:
-                    gather(d, k)
-                    if d == 2:
-                        logs(k)
-            if 0 <= step - 3 < last - 1:
-                damped(step - 3)
+        for t in range(PACK):
+            for cols in halves:
+                nc.vector.tensor_copy(g1[t][:, cols], picked(0, t, cols))
+            for cols in halves:
+                nc.vector.tensor_tensor(g2[t][:, cols], picked(1, t, cols), g1[t][:, cols], ALU.mult)
+            for cols in halves:
+                nc.vector.tensor_tensor(z[t][:, cols], picked(2, t, cols), g2[t][:, cols], ALU.mult)
+            for cols in (halves if t == PACK - 1 else [slice(0, V)]):
+                logs(t, cols)
+        for t in range(PACK - 1):
+            damped(t, slice(0, V))
 
         woven = [keep.tile([P, HALF * PACK], BF16, name="woven%d" % c, align_bytes=64) for c in range(2)]
         rr_c = [keep.tile([P, HALF], U32, name="rr_c%d" % c, align_bytes=64) for c in range(2)]
@@ -155,9 +147,10 @@ def tile_picked_yldpc_bp_p_kernel(tc, x_words, x_scales, w1, w2, damp, offs, pos
             nc.scalar.copy(res[c][:], acc[:])
             nc.sync.dma_start(out[:, c * HALF : (c + 1) * HALF], res[c][:])
 
-        damped(last - 1)
+        damped(PACK - 1, halves[0])
+        nc.vector.quantize_mx(out=w2_c[:].bitcast(FP8X4), scales=w2_s[:], in_=w2_bf[:])
         weave(0)
-        damped(last)
+        damped(PACK - 1, halves[1])
         second_product(0)
         weave(1)
         second_product(1)

@@ -20,6 +20,7 @@ PACK = 4
 GROUP = 8
 RUN = 4
 HALF = V // 2
+BLOCKS = P // GROUP
 
 
 def tile_picked_yldpc_bp_p_kernel(tc, x_words, x_scales, w1, w2, damp, offs, pos1, pos2, pos3, out):
@@ -68,12 +69,12 @@ def tile_picked_yldpc_bp_p_kernel(tc, x_words, x_scales, w1, w2, damp, offs, pos
         w1_s = [keep.tile([P, P], U8, name="w1_s%d" % t, align_bytes=64) for t in range(PACK)]
         h = [keep.tile([P, S], F32, name="h%d" % t, align_bytes=64) for t in range(PACK)]
 
-        def cast_w1(t):
+        def cast_w1(copy, t, blocks):
             dst = w1_bf[t][:].rearrange("p (b u i j) -> p b u j i", u=GROUP // RUN, i=RUN, j=PACK)
-            if t in (0, PACK - 1):
-                nc.vector.tensor_copy(dst, w1_cols[:, t])
-            else:
-                nc.scalar.copy(dst, w1_cols[:, t])
+            copy(dst[:, blocks], w1_cols[:, t, blocks])
+
+        def quantise_w1(t):
+            nc.vector.quantize_mx(out=w1_c[t][:].bitcast(FP8X4), scales=w1_s[t][:], in_=w1_bf[t][:])
 
         def first_product(t, cols, name):
             pre = psum.tile([P, cols.stop - cols.start], F32, name=name)
@@ -81,29 +82,26 @@ def tile_picked_yldpc_bp_p_kernel(tc, x_words, x_scales, w1, w2, damp, offs, pos
                                 rhs=xg_w[:, cols].bitcast(FP8X4), rhs_scale=xg_s[:, cols], start=True, stop=True)
             return pre
 
-        for t in range(PACK - 1):
-            cast_w1(t)
-        for t in range(PACK):
-            if t == 1:
-                cast_w1(PACK - 1)
-            nc.vector.quantize_mx(out=w1_c[t][:].bitcast(FP8X4), scales=w1_s[t][:], in_=w1_bf[t][:])
-        parts = [(0, slice(0, S // 2)), (0, slice(S // 2, S))] + [(t, slice(0, S)) for t in range(1, PACK)]
+        all_blocks = slice(0, BLOCKS)
+        cast_w1(nc.vector.tensor_copy, 0, slice(0, BLOCKS // 2))
+        cast_w1(nc.scalar.copy, 0, slice(BLOCKS // 2, BLOCKS))
+        cast_w1(nc.scalar.copy, 1, all_blocks)
+        cast_w1(nc.scalar.copy, 2, all_blocks)
+        quantise_w1(0)
+        cast_w1(nc.vector.tensor_copy, 3, all_blocks)
+        for t in range(1, PACK):
+            quantise_w1(t)
+        parts = [(0, slice(0, S // 4)), (0, slice(S // 4, S // 2)), (0, slice(S // 2, S))] + [(t, slice(0, S)) for t in range(1, PACK)]
         pres = [first_product(t, cols, "pre%d" % k) for k, (t, cols) in enumerate(parts)]
         for pre, (t, cols) in zip(pres, parts):
             nc.scalar.activation(h[t][:, cols], pre[:], ACT.Tanh, scale=0.5)
-
-        w2_bf = w1_bf[PACK - 2]
-        w2_c = keep.tile([P, N], U32, name="w2_c", align_bytes=64)
-        w2_s = keep.tile([P, N], U8, name="w2_s", align_bytes=64)
-        nc.scalar.copy(w2_bf[:].rearrange("p (c i t) -> p c t i", i=RUN, t=PACK),
-                              w2_raw[:].rearrange("p t (c i) -> p c t i", i=RUN))
 
         halves = [slice(c * HALF, (c + 1) * HALF) for c in range(2)]
         g1 = [keep.tile([P, V], F32, name="g1_%d" % t, align_bytes=64) for t in range(PACK)]
         g2 = [keep.tile([P, V], F32, name="g2_%d" % t, align_bytes=64) for t in range(PACK)]
         z = [keep.tile([P, V], F32, name="z%d" % t, align_bytes=64) for t in range(PACK)]
         lp = [keep.tile([P, V], F32, name="lp%d" % t, align_bytes=64) for t in range(PACK)]
-        lm = [keep.tile([P, V], F32, name="lm%d" % t, align_bytes=64) for t in range(PACK)]
+        lm = [keep.tile([P, V], F32, name="lm%d" % t, tag="lm%d" % t, align_bytes=64) for t in range(PACK)]
         lmd = [keep.tile([P, V], F32, name="lmd%d" % t, align_bytes=64) for t in range(PACK)]
         rr = keep.tile([P, PACK, V], BF16, name="rr", align_bytes=64)
 
@@ -127,6 +125,12 @@ def tile_picked_yldpc_bp_p_kernel(tc, x_words, x_scales, w1, w2, damp, offs, pos
                 nc.vector.tensor_tensor(z[t][:, cols], picked(2, t, cols), g2[t][:, cols], ALU.mult)
             for cols in (halves if t == PACK - 1 else [slice(0, V)]):
                 logs(t, cols)
+        w2_bf = keep.tile([P, N * PACK], BF16, name="w2_bf", tag="lm%d" % (PACK - 1), align_bytes=64)
+        w2_c = keep.tile([P, N], U32, name="w2_c", align_bytes=64)
+        w2_s = keep.tile([P, N], U8, name="w2_s", align_bytes=64)
+        nc.scalar.copy(w2_bf[:].rearrange("p (c i t) -> p c t i", i=RUN, t=PACK),
+                              w2_raw[:].rearrange("p t (c i) -> p c t i", i=RUN))
+
         for t in range(PACK - 1):
             damped(t, slice(0, V))
 
@@ -139,18 +143,22 @@ def tile_picked_yldpc_bp_p_kernel(tc, x_words, x_scales, w1, w2, damp, offs, pos
             nc.vector.tensor_copy(woven[c][:].rearrange("p (c i t) -> p c t i", i=RUN, t=PACK),
                                   rr[:, :, c * HALF : (c + 1) * HALF].rearrange("p t (c i) -> p c t i", i=RUN))
 
-        def second_product(c):
-            acc = psum.tile([P, HALF], F32, name="acc%d" % c)
+        def quantise_rr(c):
             nc.vector.quantize_mx(out=rr_c[c][:].bitcast(FP8X4), scales=rr_s[c][:], in_=woven[c][:])
+
+        def second_product(copy, c):
+            acc = psum.tile([P, HALF], F32, name="acc%d" % c)
             nc.tensor.matmul_mx(out=acc[:], lhsT=w2_c[:].bitcast(FP8X4), lhsT_scale=w2_s[:],
                                 rhs=rr_c[c][:].bitcast(FP8X4), rhs_scale=rr_s[c][:], start=True, stop=True)
-            nc.scalar.copy(res[c][:], acc[:])
-            nc.sync.dma_start(out[:, c * HALF : (c + 1) * HALF], res[c][:])
+            copy(res[c][:], acc[:])
+            nc.sync.dma_start(out[:, halves[c]], res[c][:])
 
         damped(PACK - 1, halves[0])
-        nc.vector.quantize_mx(out=w2_c[:].bitcast(FP8X4), scales=w2_s[:], in_=w2_bf[:])
         weave(0)
         damped(PACK - 1, halves[1])
-        second_product(0)
+        quantise_rr(0)
         weave(1)
-        second_product(1)
+        nc.vector.quantize_mx(out=w2_c[:].bitcast(FP8X4), scales=w2_s[:], in_=w2_bf[:])
+        quantise_rr(1)
+        second_product(nc.scalar.copy, 0)
+        second_product(nc.vector.tensor_copy, 1)

@@ -116,15 +116,17 @@ def tile_picked_yldpc_bp_p_kernel(tc, x_words, x_scales, w1, w2, damp, offs, pos
         def damped(t, cols):
             nc.vector.scalar_tensor_tensor(rr[:, t, cols], lp[t][:, cols], damp_pad[:, t, 0:1], lmd[t][:, cols], ALU.mult, ALU.subtract)
 
-        for t in range(PACK):
-            for cols in halves:
+        whole = slice(0, V)
+        pairs = [[(0, cols) for cols in halves], [(1, whole), (2, whole)], [(3, cols) for cols in halves]]
+        for pair in pairs:
+            for t, cols in pair:
                 nc.vector.tensor_copy(g1[t][:, cols], picked(0, t, cols))
-            for cols in halves:
+            for t, cols in pair:
                 nc.vector.tensor_tensor(g2[t][:, cols], picked(1, t, cols), g1[t][:, cols], ALU.mult)
-            for cols in halves:
+            for t, cols in pair:
                 nc.vector.tensor_tensor(z[t][:, cols], picked(2, t, cols), g2[t][:, cols], ALU.mult)
-            for cols in (halves if t == PACK - 1 else [slice(0, V)]):
-                logs(t, cols)
+        for t, cols in [(0, whole)] + pairs[1] + pairs[2]:
+            logs(t, cols)
         w2_bf = keep.tile([P, N * PACK], BF16, name="w2_bf", tag="lm%d" % (PACK - 1), align_bytes=64)
         w2_c = keep.tile([P, N], U32, name="w2_c", align_bytes=64)
         w2_s = keep.tile([P, N], U8, name="w2_s", align_bytes=64)

@@ -77,29 +77,31 @@ def tile_picked_yldpc_bp_p_kernel(tc, x_words, x_scales, w1, w2, damp, offs, pos
             nc.vector.quantize_mx(out=w1_c[t][:].bitcast(FP8X4), scales=w1_s[t][:], in_=w1_bf[t][:])
 
         def first_product(t, cols, name):
-            pre = psum.tile([P, cols.stop - cols.start], F32, name=name)
+            pre = psum.tile([P, cols.stop - cols.start], F32, name=name, tag=name)
             nc.tensor.matmul_mx(out=pre[:], lhsT=w1_c[t][:].bitcast(FP8X4), lhsT_scale=w1_s[t][:],
                                 rhs=xg_w[:, cols].bitcast(FP8X4), rhs_scale=xg_s[:, cols], start=True, stop=True)
             return pre
 
         all_blocks = slice(0, BLOCKS)
-        cast_w1(nc.vector.tensor_copy, 0, slice(0, BLOCKS // 2))
-        cast_w1(nc.scalar.copy, 0, slice(BLOCKS // 2, BLOCKS))
+        cast_w1(nc.vector.tensor_copy, 0, slice(0, 10))
+        cast_w1(nc.scalar.copy, 0, slice(10, BLOCKS))
         cast_w1(nc.scalar.copy, 1, all_blocks)
-        cast_w1(nc.scalar.copy, 2, all_blocks)
         quantise_w1(0)
+        cast_w1(nc.vector.tensor_copy, 2, all_blocks)
         cast_w1(nc.vector.tensor_copy, 3, all_blocks)
         for t in range(1, PACK):
             quantise_w1(t)
-        parts = [(0, slice(0, S // 4)), (0, slice(S // 4, S // 2)), (0, slice(S // 2, S))] + [(t, slice(0, S)) for t in range(1, PACK)]
+        parts = [(0, slice(c * P, (c + 1) * P)) for c in range(S // P)] + [(t, slice(0, S)) for t in range(1, PACK)]
         pres = [first_product(t, cols, "pre%d" % k) for k, (t, cols) in enumerate(parts)]
+        half = keep.tile([P, 8], F32, name="half", tag="hold", align_bytes=64)
+        nc.vector.memset(half[:, 0:1], 0.5)
         for pre, (t, cols) in zip(pres, parts):
-            nc.scalar.activation(h[t][:, cols], pre[:], ACT.Tanh, scale=0.5)
+            nc.scalar.activation(h[t][:, cols], pre[:], ACT.Tanh, scale=half[:, 0:1] if t == 2 else 0.5)
 
         halves = [slice(c * HALF, (c + 1) * HALF) for c in range(2)]
         g1 = [keep.tile([P, V], F32, name="g1_%d" % t, align_bytes=64) for t in range(PACK)]
-        g2 = [keep.tile([P, V], F32, name="g2_%d" % t, align_bytes=64) for t in range(PACK)]
-        z = [keep.tile([P, V], F32, name="z%d" % t, align_bytes=64) for t in range(PACK)]
+        g2 = [keep.tile([P, V], F32, name="g2_%d" % t, tag="hold" if t == 1 else "g2_%d" % t, align_bytes=64) for t in range(PACK)]
+        z = [keep.tile([P, V], F32, name="z%d" % t, tag="z%d" % t, align_bytes=64) for t in range(PACK)]
         lp = [keep.tile([P, V], F32, name="lp%d" % t, align_bytes=64) for t in range(PACK)]
         lm = [keep.tile([P, V], F32, name="lm%d" % t, tag="lm%d" % t, align_bytes=64) for t in range(PACK)]
         lmd = [keep.tile([P, V], F32, name="lmd%d" % t, align_bytes=64) for t in range(PACK)]
@@ -117,16 +119,30 @@ def tile_picked_yldpc_bp_p_kernel(tc, x_words, x_scales, w1, w2, damp, offs, pos
             nc.vector.scalar_tensor_tensor(rr[:, t, cols], lp[t][:, cols], damp_pad[:, t, 0:1], lmd[t][:, cols], ALU.mult, ALU.subtract)
 
         whole = slice(0, V)
-        pairs = [[(0, cols) for cols in halves], [(1, whole), (2, whole)], [(3, cols) for cols in halves]]
-        for pair in pairs:
-            for t, cols in pair:
-                nc.vector.tensor_copy(g1[t][:, cols], picked(0, t, cols))
-            for t, cols in pair:
-                nc.vector.tensor_tensor(g2[t][:, cols], picked(1, t, cols), g1[t][:, cols], ALU.mult)
-            for t, cols in pair:
-                nc.vector.tensor_tensor(z[t][:, cols], picked(2, t, cols), g2[t][:, cols], ALU.mult)
-        for t, cols in [(0, whole)] + pairs[1] + pairs[2]:
-            logs(t, cols)
+
+        def first(t, cols):
+            nc.vector.tensor_copy(g1[t][:, cols], picked(0, t, cols))
+
+        def second(t, cols):
+            nc.vector.tensor_tensor(g2[t][:, cols], picked(1, t, cols), g1[t][:, cols], ALU.mult)
+
+        def third(t, cols):
+            nc.vector.tensor_tensor(z[t][:, cols], picked(2, t, cols), g2[t][:, cols], ALU.mult)
+
+        for step in (first, second, third):
+            for cols in halves:
+                step(0, cols)
+        for step in (first, second, third):
+            for t in (1, 2):
+                step(t, whole)
+        for step in (first, second, third):
+            for cols in halves:
+                step(3, cols)
+        logs(0, whole)
+        logs(1, whole)
+        logs(2, whole)
+        for cols in halves:
+            logs(3, cols)
         w2_bf = keep.tile([P, N * PACK], BF16, name="w2_bf", tag="lm%d" % (PACK - 1), align_bytes=64)
         w2_c = keep.tile([P, N], U32, name="w2_c", align_bytes=64)
         w2_s = keep.tile([P, N], U8, name="w2_s", align_bytes=64)
@@ -141,25 +157,25 @@ def tile_picked_yldpc_bp_p_kernel(tc, x_words, x_scales, w1, w2, damp, offs, pos
         rr_s = [keep.tile([P, HALF], U8, name="rr_s%d" % c, align_bytes=64) for c in range(2)]
         res = [keep.tile([P, HALF], F32, name="res%d" % c, align_bytes=64) for c in range(2)]
 
-        def weave(c):
-            nc.vector.tensor_copy(woven[c][:].rearrange("p (c i t) -> p c t i", i=RUN, t=PACK),
+        def weave(copy, c):
+            copy(woven[c][:].rearrange("p (c i t) -> p c t i", i=RUN, t=PACK),
                                   rr[:, :, c * HALF : (c + 1) * HALF].rearrange("p t (c i) -> p c t i", i=RUN))
 
         def quantise_rr(c):
             nc.vector.quantize_mx(out=rr_c[c][:].bitcast(FP8X4), scales=rr_s[c][:], in_=woven[c][:])
 
         def second_product(copy, c):
-            acc = psum.tile([P, HALF], F32, name="acc%d" % c)
+            acc = psum.tile([P, HALF], F32, name="acc%d" % c, tag="pre%d" % c)
             nc.tensor.matmul_mx(out=acc[:], lhsT=w2_c[:].bitcast(FP8X4), lhsT_scale=w2_s[:],
                                 rhs=rr_c[c][:].bitcast(FP8X4), rhs_scale=rr_s[c][:], start=True, stop=True)
             copy(res[c][:], acc[:])
             nc.sync.dma_start(out[:, halves[c]], res[c][:])
 
         damped(PACK - 1, halves[0])
-        weave(0)
+        weave(nc.vector.tensor_copy, 0)
         damped(PACK - 1, halves[1])
         quantise_rr(0)
-        weave(1)
+        weave(nc.vector.tensor_copy, 1)
         nc.vector.quantize_mx(out=w2_c[:].bitcast(FP8X4), scales=w2_s[:], in_=w2_bf[:])
         quantise_rr(1)
         second_product(nc.scalar.copy, 0)

@@ -99,8 +99,8 @@ def tile_picked_yldpc_bp_p_kernel(tc, x_words, x_scales, w1, w2, damp, offs, pos
             nc.scalar.activation(h[t][:, cols], pre[:], ACT.Tanh, scale=half[:, 0:1] if t == 2 else 0.5)
 
         halves = [slice(c * HALF, (c + 1) * HALF) for c in range(2)]
-        g1 = [keep.tile([P, V], F32, name="g1_%d" % t, align_bytes=64) for t in range(PACK)]
-        g2 = [keep.tile([P, V], F32, name="g2_%d" % t, tag="hold" if t == 1 else "g2_%d" % t, align_bytes=64) for t in range(PACK)]
+        g1 = [keep.tile([P, V], F32, name="g1_%d" % t, tag="hold" if t == 1 else "g1_%d" % t, align_bytes=64) for t in range(PACK)]
+        g2 = [keep.tile([P, V], F32, name="g2_%d" % t, align_bytes=64) for t in range(PACK)]
         z = [keep.tile([P, V], F32, name="z%d" % t, tag="z%d" % t, align_bytes=64) for t in range(PACK)]
         lp = [keep.tile([P, V], F32, name="lp%d" % t, align_bytes=64) for t in range(PACK)]
         lm = [keep.tile([P, V], F32, name="lm%d" % t, tag="lm%d" % t, align_bytes=64) for t in range(PACK)]
@@ -133,14 +133,14 @@ def tile_picked_yldpc_bp_p_kernel(tc, x_words, x_scales, w1, w2, damp, offs, pos
             for cols in halves:
                 step(0, cols)
         for step in (first, second, third):
-            for t in (1, 2):
+            for t in (2, 1):
                 step(t, whole)
         for step in (first, second, third):
             for cols in halves:
                 step(3, cols)
         logs(0, whole)
-        logs(1, whole)
         logs(2, whole)
+        logs(1, whole)
         for cols in halves:
             logs(3, cols)
         w2_bf = keep.tile([P, N * PACK], BF16, name="w2_bf", tag="lm%d" % (PACK - 1), align_bytes=64)
@@ -149,7 +149,7 @@ def tile_picked_yldpc_bp_p_kernel(tc, x_words, x_scales, w1, w2, damp, offs, pos
         nc.scalar.copy(w2_bf[:].rearrange("p (c i t) -> p c t i", i=RUN, t=PACK),
                               w2_raw[:].rearrange("p t (c i) -> p c t i", i=RUN))
 
-        for t in range(PACK - 1):
+        for t in (0, 2, 1):
             damped(t, slice(0, V))
 
         woven = [keep.tile([P, HALF * PACK], BF16, name="woven%d" % c, align_bytes=64) for c in range(2)]

@@ -27,13 +27,14 @@ def tile_picked_yldpc_bp_p_kernel(tc, x_words, x_scales, w1, w2, damp, offs, pos
     nc = tc.nc
     with ExitStack() as ctx:
         keep = ctx.enter_context(tc.tile_pool(name="keep", bufs=1))
+        lap = ctx.enter_context(tc.tile_pool(name="lap", bufs=1))
         psum = ctx.enter_context(tc.psum_pool(name="psum", bufs=1))
 
         offs_t = keep.tile([P, S // 16], U16, name="offs_t")
         pos_t = [keep.tile([P, V // 16], U16, name="pos_t%d" % d) for d in range(3)]
         xw = keep.tile([P, T], U32, name="xw", align_bytes=64)
         xs = keep.tile([P, T], U8, name="xs", align_bytes=64)
-        w1_raw = keep.tile([P, PACK, H], F32, name="w1_raw", align_bytes=64)
+        w1_raw = [keep.tile([P, PACK, H // 2], F32, name="w1_raw%d" % c, align_bytes=64) for c in range(2)]
         w2_raw = keep.tile([P, PACK, N], F32, name="w2_raw", align_bytes=64)
         damp_pad = keep.tile([P, PACK, 8], F32, name="damp_pad", align_bytes=64)
         warm = keep.tile([P, 8], F32, name="warm", align_bytes=64)
@@ -41,37 +42,38 @@ def tile_picked_yldpc_bp_p_kernel(tc, x_words, x_scales, w1, w2, damp, offs, pos
 
         nc.vector.memset(xs[:].bitcast(I32), 0)
         nc.vector.memset(warm[:], 0.0)
-        nc.sync.dma_start(xw[:].bitcast(I32), x_words[0].rearrange("p n t -> p (n t)").bitcast(I32))
         nc.sync.dma_start(offs_t[:], offs)
+        nc.sync.dma_start(xw[:].bitcast(I32), x_words[0].rearrange("p n t -> p (n t)").bitcast(I32))
         nc.sync.dma_start(pos_t[0][:], pos1)
         for q in range(4):
             nc.sync.dma_start(xs[32 * q : 32 * q + 4, :].bitcast(I32), x_scales[0, 4 * q : 4 * q + 4, :].bitcast(I32))
-        nc.sync.dma_start(w1_raw[:], w1.rearrange("(p j) c -> p j c", j=PACK))
+        w1_rows = w1.rearrange("(p j) c -> p j c", j=PACK)
+        for c in range(2):
+            nc.sync.dma_start(w1_raw[c][:], w1_rows[:, :, c * (H // 2) : (c + 1) * (H // 2)])
         nc.scalar.activation(warm_out[:], warm[:], ACT.Tanh, scale=0.5)
-        nc.sync.dma_start(pos_t[1][:], pos2)
-        nc.sync.dma_start(pos_t[2][:], pos3)
         w2_rows = w2.rearrange("(b t r) n -> t b r n", t=PACK, r=GROUP)
         for t in range(PACK):
             nc.sync.dma_start(w2_raw[:, t, :], w2_rows[t])
+        nc.sync.dma_start(pos_t[1][:], pos2)
+        nc.sync.dma_start(pos_t[2][:], pos3)
         damp_rows = damp.rearrange("(b t r) o -> t b r o", t=PACK, r=GROUP)
         for t in range(PACK):
             nc.sync.dma_start(damp_pad[:, t, 0:1], damp_rows[t])
 
         xg_s = keep.tile([P, S], U8, name="xg_s", align_bytes=64)
         xg_w = keep.tile([P, S], U32, name="xg_w", align_bytes=64)
-        nc.vector.tensor_copy(xg_s[:], xs[:].indirect(offs_t[:]))
         nc.vector.tensor_copy(xg_w[:], xw[:].indirect(offs_t[:]))
+        nc.vector.tensor_copy(xg_s[:], xs[:].indirect(offs_t[:]))
 
-        w1_cols = w1_raw[:].rearrange("p j (b t u i) -> p t b u j i", t=PACK, u=GROUP // RUN, i=RUN)
-        w1_bf = [keep.tile([P, P * PACK], BF16, name="w1_bf%d" % t, align_bytes=64) for t in range(PACK - 1)]
-        w1_bf.append(w1_bf[0])
+        w1_cols = [w1_raw[c][:].rearrange("p j (b t u i) -> p t b u j i", t=PACK, u=GROUP // RUN, i=RUN) for c in range(2)]
+        w1_bf = [keep.tile([P, P * PACK], BF16, name="w1_bf%d" % t, align_bytes=64) for t in range(PACK)]
         w1_c = [keep.tile([P, P], U32, name="w1_c%d" % t, align_bytes=64) for t in range(PACK)]
         w1_s = [keep.tile([P, P], U8, name="w1_s%d" % t, align_bytes=64) for t in range(PACK)]
         h = [keep.tile([P, S], F32, name="h%d" % t, align_bytes=64) for t in range(PACK)]
 
-        def cast_w1(copy, t, blocks):
-            dst = w1_bf[t][:].rearrange("p (b u i j) -> p b u j i", u=GROUP // RUN, i=RUN, j=PACK)
-            copy(dst[:, blocks], w1_cols[:, t, blocks])
+        def cast_w1(copy, t, c):
+            dst = w1_bf[t][:].rearrange("p (c b u i j) -> p c b u j i", c=2, u=GROUP // RUN, i=RUN, j=PACK)
+            copy(dst[:, c], w1_cols[c][:, t])
 
         def quantise_w1(t):
             nc.vector.quantize_mx(out=w1_c[t][:].bitcast(FP8X4), scales=w1_s[t][:], in_=w1_bf[t][:])
@@ -82,25 +84,31 @@ def tile_picked_yldpc_bp_p_kernel(tc, x_words, x_scales, w1, w2, damp, offs, pos
                                 rhs=xg_w[:, cols].bitcast(FP8X4), rhs_scale=xg_s[:, cols], start=True, stop=True)
             return pre
 
-        all_blocks = slice(0, BLOCKS)
-        cast_w1(nc.vector.tensor_copy, 0, slice(0, 10))
-        cast_w1(nc.scalar.copy, 0, slice(10, BLOCKS))
-        cast_w1(nc.scalar.copy, 1, all_blocks)
+        w2_bf = lap.tile([P, N * PACK], BF16, name="w2_bf", align_bytes=64, offset=512)
+        w2_c = keep.tile([P, N], U32, name="w2_c", align_bytes=64)
+        w2_s = keep.tile([P, N], U8, name="w2_s", align_bytes=64)
+
+        for t in range(PACK):
+            cast_w1(nc.scalar.copy, t, 0)
+        cast_w1(nc.scalar.copy, 3, 1)
+        cast_w1(nc.vector.tensor_copy, 0, 1)
+        cast_w1(nc.vector.tensor_copy, 1, 1)
         quantise_w1(0)
-        cast_w1(nc.vector.tensor_copy, 2, all_blocks)
-        cast_w1(nc.vector.tensor_copy, 3, all_blocks)
+        cast_w1(nc.vector.tensor_copy, 2, 1)
         for t in range(1, PACK):
             quantise_w1(t)
-        parts = [(0, slice(c * P, (c + 1) * P)) for c in range(S // P)] + [(t, slice(0, S)) for t in range(1, PACK)]
+        nc.vector.tensor_copy(w2_bf[:].rearrange("p (c i t) -> p c t i", i=RUN, t=PACK),
+                              w2_raw[:].rearrange("p t (c i) -> p c t i", i=RUN))
+        nc.vector.quantize_mx(out=w2_c[:].bitcast(FP8X4), scales=w2_s[:], in_=w2_bf[:])
+        edges = [(0, 128, 256, 512), (0, 256, 512), (0, 256, 512), (0, 512)]
+        parts = [(t, slice(a, b)) for t in range(PACK) for a, b in zip(edges[t], edges[t][1:])]
         pres = [first_product(t, cols, "pre%d" % k) for k, (t, cols) in enumerate(parts)]
-        half = keep.tile([P, 8], F32, name="half", tag="hold", align_bytes=64)
-        nc.vector.memset(half[:, 0:1], 0.5)
         for pre, (t, cols) in zip(pres, parts):
-            nc.scalar.activation(h[t][:, cols], pre[:], ACT.Tanh, scale=half[:, 0:1] if t == 2 else 0.5)
+            nc.scalar.activation(h[t][:, cols], pre[:], ACT.Tanh, scale=0.5)
 
         halves = [slice(c * HALF, (c + 1) * HALF) for c in range(2)]
-        g1 = [keep.tile([P, V], F32, name="g1_%d" % t, tag="hold" if t == 1 else "g1_%d" % t, align_bytes=64) for t in range(PACK)]
-        g2 = [keep.tile([P, V], F32, name="g2_%d" % t, align_bytes=64) for t in range(PACK)]
+        g1 = [lap.tile([P, V], F32, name="g1_%d" % t, align_bytes=64, offset=(0, 1024, 1024, 2048)[t]) for t in range(PACK)]
+        g2 = [lap.tile([P, V], F32, name="g2_%d" % t, align_bytes=64, offset=(3072, 2048, 4096, 5120)[t]) for t in range(PACK)]
         z = [keep.tile([P, V], F32, name="z%d" % t, tag="z%d" % t, align_bytes=64) for t in range(PACK)]
         lp = [keep.tile([P, V], F32, name="lp%d" % t, align_bytes=64) for t in range(PACK)]
         lm = [keep.tile([P, V], F32, name="lm%d" % t, tag="lm%d" % t, align_bytes=64) for t in range(PACK)]
@@ -129,28 +137,25 @@ def tile_picked_yldpc_bp_p_kernel(tc, x_words, x_scales, w1, w2, damp, offs, pos
         def third(t, cols):
             nc.vector.tensor_tensor(z[t][:, cols], picked(2, t, cols), g2[t][:, cols], ALU.mult)
 
-        for step in (first, second, third):
-            for cols in halves:
-                step(0, cols)
-        for step in (first, second, third):
-            for t in (2, 1):
-                step(t, whole)
-        for step in (first, second, third):
+        first(0, whole)
+        first(1, whole)
+        second(0, whole)
+        second(1, whole)
+        third(0, whole)
+        first(2, whole)
+        third(1, whole)
+        second(2, whole)
+        first(3, whole)
+        third(2, whole)
+        for step in (second, third):
             for cols in halves:
                 step(3, cols)
-        logs(0, whole)
-        logs(2, whole)
-        logs(1, whole)
+        for t in range(PACK - 1):
+            logs(t, whole)
         for cols in halves:
             logs(3, cols)
-        w2_bf = keep.tile([P, N * PACK], BF16, name="w2_bf", tag="lm%d" % (PACK - 1), align_bytes=64)
-        w2_c = keep.tile([P, N], U32, name="w2_c", align_bytes=64)
-        w2_s = keep.tile([P, N], U8, name="w2_s", align_bytes=64)
-        nc.scalar.copy(w2_bf[:].rearrange("p (c i t) -> p c t i", i=RUN, t=PACK),
-                              w2_raw[:].rearrange("p t (c i) -> p c t i", i=RUN))
-
-        for t in (0, 2, 1):
-            damped(t, slice(0, V))
+        for t in range(PACK - 1):
+            damped(t, whole)
 
         woven = [keep.tile([P, HALF * PACK], BF16, name="woven%d" % c, align_bytes=64) for c in range(2)]
         rr_c = [keep.tile([P, HALF], U32, name="rr_c%d" % c, align_bytes=64) for c in range(2)]
@@ -176,7 +181,6 @@ def tile_picked_yldpc_bp_p_kernel(tc, x_words, x_scales, w1, w2, damp, offs, pos
         damped(PACK - 1, halves[1])
         quantise_rr(0)
         weave(nc.vector.tensor_copy, 1)
-        nc.vector.quantize_mx(out=w2_c[:].bitcast(FP8X4), scales=w2_s[:], in_=w2_bf[:])
         quantise_rr(1)
         second_product(nc.scalar.copy, 0)
         second_product(nc.vector.tensor_copy, 1)

@@ -34,28 +34,28 @@ def tile_picked_yldpc_bp_p_kernel(tc, x_words, x_scales, w1, w2, damp, offs, pos
         pos_t = [keep.tile([P, V // 16], U16, name="pos_t%d" % d) for d in range(3)]
         xw = keep.tile([P, T], U32, name="xw", align_bytes=64)
         xs = keep.tile([P, T], U8, name="xs", align_bytes=64)
-        w1_raw = [keep.tile([P, PACK, H // 2], F32, name="w1_raw%d" % c, align_bytes=64) for c in range(2)]
+        w1_raw = keep.tile([P, PACK, H], F32, name="w1_raw", align_bytes=64)
         w2_raw = keep.tile([P, PACK, N], F32, name="w2_raw", align_bytes=64)
         damp_pad = keep.tile([P, PACK, 8], F32, name="damp_pad", align_bytes=64)
         warm = keep.tile([P, 8], F32, name="warm", align_bytes=64)
         warm_out = keep.tile([P, 8], F32, name="warm_out", align_bytes=64)
 
+        zero = lap.tile([P, 32], F32, name="zero", align_bytes=64, offset=3072 - 64)
         nc.vector.memset(xs[:].bitcast(I32), 0)
         nc.vector.memset(warm[:], 0.0)
-        nc.sync.dma_start(offs_t[:], offs)
+        nc.vector.memset(zero[:], 0.0)
         nc.sync.dma_start(xw[:].bitcast(I32), x_words[0].rearrange("p n t -> p (n t)").bitcast(I32))
+        nc.sync.dma_start(offs_t[:], offs)
         nc.sync.dma_start(pos_t[0][:], pos1)
         for q in range(4):
             nc.sync.dma_start(xs[32 * q : 32 * q + 4, :].bitcast(I32), x_scales[0, 4 * q : 4 * q + 4, :].bitcast(I32))
-        w1_rows = w1.rearrange("(p j) c -> p j c", j=PACK)
-        for c in range(2):
-            nc.sync.dma_start(w1_raw[c][:], w1_rows[:, :, c * (H // 2) : (c + 1) * (H // 2)])
+        nc.sync.dma_start(w1_raw[:], w1.rearrange("(p j) c -> p j c", j=PACK))
         nc.scalar.activation(warm_out[:], warm[:], ACT.Tanh, scale=0.5)
+        nc.sync.dma_start(pos_t[1][:], pos2)
+        nc.sync.dma_start(pos_t[2][:], pos3)
         w2_rows = w2.rearrange("(b t r) n -> t b r n", t=PACK, r=GROUP)
         for t in range(PACK):
             nc.sync.dma_start(w2_raw[:, t, :], w2_rows[t])
-        nc.sync.dma_start(pos_t[1][:], pos2)
-        nc.sync.dma_start(pos_t[2][:], pos3)
         damp_rows = damp.rearrange("(b t r) o -> t b r o", t=PACK, r=GROUP)
         for t in range(PACK):
             nc.sync.dma_start(damp_pad[:, t, 0:1], damp_rows[t])
@@ -65,15 +65,16 @@ def tile_picked_yldpc_bp_p_kernel(tc, x_words, x_scales, w1, w2, damp, offs, pos
         nc.vector.tensor_copy(xg_w[:], xw[:].indirect(offs_t[:]))
         nc.vector.tensor_copy(xg_s[:], xs[:].indirect(offs_t[:]))
 
-        w1_cols = [w1_raw[c][:].rearrange("p j (b t u i) -> p t b u j i", t=PACK, u=GROUP // RUN, i=RUN) for c in range(2)]
-        w1_bf = [keep.tile([P, P * PACK], BF16, name="w1_bf%d" % t, align_bytes=64) for t in range(PACK)]
+        w1_cols = w1_raw[:].rearrange("p j (b t u i) -> p t b u j i", t=PACK, u=GROUP // RUN, i=RUN)
+        w1_bf = [keep.tile([P, P * PACK], BF16, name="w1_bf%d" % t, align_bytes=64) for t in range(PACK - 1)]
+        w1_bf.append(w1_bf[0])
         w1_c = [keep.tile([P, P], U32, name="w1_c%d" % t, align_bytes=64) for t in range(PACK)]
         w1_s = [keep.tile([P, P], U8, name="w1_s%d" % t, align_bytes=64) for t in range(PACK)]
         h = [keep.tile([P, S], F32, name="h%d" % t, align_bytes=64) for t in range(PACK)]
 
-        def cast_w1(copy, t, c):
-            dst = w1_bf[t][:].rearrange("p (c b u i j) -> p c b u j i", c=2, u=GROUP // RUN, i=RUN, j=PACK)
-            copy(dst[:, c], w1_cols[c][:, t])
+        def cast_w1(copy, t, blocks):
+            dst = w1_bf[t][:].rearrange("p (b u i j) -> p b u j i", u=GROUP // RUN, i=RUN, j=PACK)
+            copy(dst[:, blocks], w1_cols[:, t, blocks])
 
         def quantise_w1(t):
             nc.vector.quantize_mx(out=w1_c[t][:].bitcast(FP8X4), scales=w1_s[t][:], in_=w1_bf[t][:])
@@ -84,27 +85,20 @@ def tile_picked_yldpc_bp_p_kernel(tc, x_words, x_scales, w1, w2, damp, offs, pos
                                 rhs=xg_w[:, cols].bitcast(FP8X4), rhs_scale=xg_s[:, cols], start=True, stop=True)
             return pre
 
-        w2_bf = lap.tile([P, N * PACK], BF16, name="w2_bf", align_bytes=64, offset=512)
-        w2_c = keep.tile([P, N], U32, name="w2_c", align_bytes=64)
-        w2_s = keep.tile([P, N], U8, name="w2_s", align_bytes=64)
-
-        for t in range(PACK):
-            cast_w1(nc.scalar.copy, t, 0)
-        cast_w1(nc.scalar.copy, 3, 1)
-        cast_w1(nc.vector.tensor_copy, 0, 1)
-        cast_w1(nc.vector.tensor_copy, 1, 1)
+        all_blocks = slice(0, BLOCKS)
+        cast_w1(nc.vector.tensor_copy, 0, slice(0, 10))
+        cast_w1(nc.scalar.copy, 0, slice(10, BLOCKS))
+        cast_w1(nc.scalar.copy, 2, all_blocks)
         quantise_w1(0)
-        cast_w1(nc.vector.tensor_copy, 2, 1)
+        cast_w1(nc.vector.tensor_copy, 1, all_blocks)
+        cast_w1(nc.vector.tensor_copy, 3, all_blocks)
         for t in range(1, PACK):
             quantise_w1(t)
-        nc.vector.tensor_copy(w2_bf[:].rearrange("p (c i t) -> p c t i", i=RUN, t=PACK),
-                              w2_raw[:].rearrange("p t (c i) -> p c t i", i=RUN))
-        nc.vector.quantize_mx(out=w2_c[:].bitcast(FP8X4), scales=w2_s[:], in_=w2_bf[:])
         edges = [(0, 128, 256, 512), (0, 256, 512), (0, 256, 512), (0, 512)]
         parts = [(t, slice(a, b)) for t in range(PACK) for a, b in zip(edges[t], edges[t][1:])]
         pres = [first_product(t, cols, "pre%d" % k) for k, (t, cols) in enumerate(parts)]
         for pre, (t, cols) in zip(pres, parts):
-            nc.scalar.activation(h[t][:, cols], pre[:], ACT.Tanh, scale=0.5)
+            nc.scalar.activation(h[t][:, cols], pre[:], ACT.Tanh, scale=0.5, bias=zero[:, 0:1] if (t, cols.start) == (2, 0) else 0.0)
 
         halves = [slice(c * HALF, (c + 1) * HALF) for c in range(2)]
         g1 = [lap.tile([P, V], F32, name="g1_%d" % t, align_bytes=64, offset=(0, 1024, 1024, 2048)[t]) for t in range(PACK)]
@@ -154,6 +148,12 @@ def tile_picked_yldpc_bp_p_kernel(tc, x_words, x_scales, w1, w2, damp, offs, pos
             logs(t, whole)
         for cols in halves:
             logs(3, cols)
+        w2_bf = keep.tile([P, N * PACK], BF16, name="w2_bf", tag="lm%d" % (PACK - 1), align_bytes=64)
+        w2_c = keep.tile([P, N], U32, name="w2_c", align_bytes=64)
+        w2_s = keep.tile([P, N], U8, name="w2_s", align_bytes=64)
+        nc.scalar.copy(w2_bf[:].rearrange("p (c i t) -> p c t i", i=RUN, t=PACK),
+                              w2_raw[:].rearrange("p t (c i) -> p c t i", i=RUN))
+
         for t in range(PACK - 1):
             damped(t, whole)
 
@@ -181,6 +181,7 @@ def tile_picked_yldpc_bp_p_kernel(tc, x_words, x_scales, w1, w2, damp, offs, pos
         damped(PACK - 1, halves[1])
         quantise_rr(0)
         weave(nc.vector.tensor_copy, 1)
+        nc.vector.quantize_mx(out=w2_c[:].bitcast(FP8X4), scales=w2_s[:], in_=w2_bf[:])
         quantise_rr(1)
         second_product(nc.scalar.copy, 0)
         second_product(nc.vector.tensor_copy, 1)

@@ -94,9 +94,9 @@ def tile_picked_yldpc_bp_p_kernel(tc, x_words, x_scales, w1, w2, damp, offs, pos
         cast_w1(nc.vector.tensor_copy, 3, all_blocks)
         for t in range(1, PACK):
             quantise_w1(t)
-        edges = [(0, 128, 256, 512), (0, 256, 512), (0, 256, 512), (0, 512)]
+        edges = [(0, 128, 256, 384, 512), (0, 256, 512), (0, 256, 512), (0, 256, 512)]
         parts = [(t, slice(a, b)) for t in range(PACK) for a, b in zip(edges[t], edges[t][1:])]
-        pres = [first_product(t, cols, "pre%d" % k) for k, (t, cols) in enumerate(parts)]
+        pres = [first_product(t, cols, "pre%d" % (k % 8)) for k, (t, cols) in enumerate(parts)]
         for pre, (t, cols) in zip(pres, parts):
             nc.scalar.activation(h[t][:, cols], pre[:], ACT.Tanh, scale=0.5, bias=zero[:, 0:1] if (t, cols.start) == (2, 0) else 0.0)
 
@@ -105,7 +105,7 @@ def tile_picked_yldpc_bp_p_kernel(tc, x_words, x_scales, w1, w2, damp, offs, pos
         g2 = [lap.tile([P, V], F32, name="g2_%d" % t, align_bytes=64, offset=(3072, 2048, 4096, 5120)[t]) for t in range(PACK)]
         z = [keep.tile([P, V], F32, name="z%d" % t, tag="z%d" % t, align_bytes=64) for t in range(PACK)]
         lp = [keep.tile([P, V], F32, name="lp%d" % t, align_bytes=64) for t in range(PACK)]
-        lm = [keep.tile([P, V], F32, name="lm%d" % t, tag="lm%d" % t, align_bytes=64) for t in range(PACK)]
+        lm = [lap.tile([P, V], F32, name="lm%d" % t, align_bytes=64, offset=(6144, 7168, 8192, 9728)[t]) for t in range(PACK)]
         lmd = [keep.tile([P, V], F32, name="lmd%d" % t, align_bytes=64) for t in range(PACK)]
         rr = keep.tile([P, PACK, V], BF16, name="rr", align_bytes=64)
 
@@ -148,7 +148,7 @@ def tile_picked_yldpc_bp_p_kernel(tc, x_words, x_scales, w1, w2, damp, offs, pos
             logs(t, whole)
         for cols in halves:
             logs(3, cols)
-        w2_bf = keep.tile([P, N * PACK], BF16, name="w2_bf", tag="lm%d" % (PACK - 1), align_bytes=64)
+        w2_bf = lap.tile([P, N * PACK], BF16, name="w2_bf", align_bytes=64, offset=9216)
         w2_c = keep.tile([P, N], U32, name="w2_c", align_bytes=64)
         w2_s = keep.tile([P, N], U8, name="w2_s", align_bytes=64)
         nc.scalar.copy(w2_bf[:].rearrange("p (c i t) -> p c t i", i=RUN, t=PACK),
@@ -157,7 +157,7 @@ def tile_picked_yldpc_bp_p_kernel(tc, x_words, x_scales, w1, w2, damp, offs, pos
         for t in range(PACK - 1):
             damped(t, whole)
 
-        woven = [keep.tile([P, HALF * PACK], BF16, name="woven%d" % c, align_bytes=64) for c in range(2)]
+        woven = [lap.tile([P, HALF * PACK], BF16, name="woven%d" % c, align_bytes=64, offset=(10240, 11264)[c]) for c in range(2)]
         rr_c = [keep.tile([P, HALF], U32, name="rr_c%d" % c, align_bytes=64) for c in range(2)]
         rr_s = [keep.tile([P, HALF], U8, name="rr_s%d" % c, align_bytes=64) for c in range(2)]
         res = [keep.tile([P, HALF], F32, name="res%d" % c, align_bytes=64) for c in range(2)]
@@ -170,17 +170,17 @@ def tile_picked_yldpc_bp_p_kernel(tc, x_words, x_scales, w1, w2, damp, offs, pos
             nc.vector.quantize_mx(out=rr_c[c][:].bitcast(FP8X4), scales=rr_s[c][:], in_=woven[c][:])
 
         def second_product(copy, c):
-            acc = psum.tile([P, HALF], F32, name="acc%d" % c, tag="pre%d" % c)
+            acc = psum.tile([P, HALF], F32, name="acc%d" % c, tag="pre%d" % (c + 2))
             nc.tensor.matmul_mx(out=acc[:], lhsT=w2_c[:].bitcast(FP8X4), lhsT_scale=w2_s[:],
                                 rhs=rr_c[c][:].bitcast(FP8X4), rhs_scale=rr_s[c][:], start=True, stop=True)
             copy(res[c][:], acc[:])
             nc.sync.dma_start(out[:, halves[c]], res[c][:])
 
-        damped(PACK - 1, halves[0])
-        weave(nc.vector.tensor_copy, 0)
-        damped(PACK - 1, halves[1])
+        for cols in halves:
+            damped(PACK - 1, cols)
+        for c in range(2):
+            weave(nc.vector.tensor_copy, c)
         quantise_rr(0)
-        weave(nc.vector.tensor_copy, 1)
         nc.vector.quantize_mx(out=w2_c[:].bitcast(FP8X4), scales=w2_s[:], in_=w2_bf[:])
         quantise_rr(1)
         second_product(nc.scalar.copy, 0)

@@ -100,6 +100,10 @@ def tile_picked_yldpc_bp_p_kernel(tc, x_words, x_scales, w1, w2, damp, offs, pos
         for pre, (t, cols) in zip(pres, parts):
             nc.scalar.activation(h[t][:, cols], pre[:], ACT.Tanh, scale=0.5, bias=zero[:, 0:1] if (t, cols.start) == (2, 0) else 0.0)
 
+        w2_bf = keep.tile([P, N * PACK], BF16, name="w2_bf", align_bytes=64)
+        nc.scalar.copy(w2_bf[:].rearrange("p (c i t) -> p c t i", i=RUN, t=PACK),
+                       w2_raw[:].rearrange("p t (c i) -> p c t i", i=RUN))
+
         halves = [slice(c * HALF, (c + 1) * HALF) for c in range(2)]
         g1 = [lap.tile([P, V], F32, name="g1_%d" % t, align_bytes=64, offset=(0, 1024, 1024, 2048)[t]) for t in range(PACK)]
         g2 = [lap.tile([P, V], F32, name="g2_%d" % t, align_bytes=64, offset=(3072, 2048, 4096, 5120)[t]) for t in range(PACK)]
@@ -144,16 +148,11 @@ def tile_picked_yldpc_bp_p_kernel(tc, x_words, x_scales, w1, w2, damp, offs, pos
         for step in (second, third):
             for cols in halves:
                 step(3, cols)
-        for t in range(PACK - 1):
-            logs(t, whole)
+        logs(0, whole)
+        logs(1, whole)
+        logs(2, whole)
         for cols in halves:
             logs(3, cols)
-        w2_bf = lap.tile([P, N * PACK], BF16, name="w2_bf", align_bytes=64, offset=9216)
-        w2_c = keep.tile([P, N], U32, name="w2_c", align_bytes=64)
-        w2_s = keep.tile([P, N], U8, name="w2_s", align_bytes=64)
-        nc.scalar.copy(w2_bf[:].rearrange("p (c i t) -> p c t i", i=RUN, t=PACK),
-                              w2_raw[:].rearrange("p t (c i) -> p c t i", i=RUN))
-
         for t in range(PACK - 1):
             damped(t, whole)
 
@@ -162,9 +161,9 @@ def tile_picked_yldpc_bp_p_kernel(tc, x_words, x_scales, w1, w2, damp, offs, pos
         rr_s = [keep.tile([P, HALF], U8, name="rr_s%d" % c, align_bytes=64) for c in range(2)]
         res = [keep.tile([P, HALF], F32, name="res%d" % c, align_bytes=64) for c in range(2)]
 
-        def weave(copy, c):
-            copy(woven[c][:].rearrange("p (c i t) -> p c t i", i=RUN, t=PACK),
-                                  rr[:, :, c * HALF : (c + 1) * HALF].rearrange("p t (c i) -> p c t i", i=RUN))
+        def weave(copy, c, a, b):
+            copy(woven[c][:, PACK * a : PACK * b].rearrange("p (c i t) -> p c t i", i=RUN, t=PACK),
+                 rr[:, :, c * HALF + a : c * HALF + b].rearrange("p t (c i) -> p c t i", i=RUN))
 
         def quantise_rr(c):
             nc.vector.quantize_mx(out=rr_c[c][:].bitcast(FP8X4), scales=rr_s[c][:], in_=woven[c][:])
@@ -178,8 +177,12 @@ def tile_picked_yldpc_bp_p_kernel(tc, x_words, x_scales, w1, w2, damp, offs, pos
 
         for cols in halves:
             damped(PACK - 1, cols)
-        for c in range(2):
-            weave(nc.vector.tensor_copy, c)
+        w2_c = lap.tile([P, N], U32, name="w2_c", align_bytes=64, offset=9728)
+        w2_s = keep.tile([P, N], U8, name="w2_s", align_bytes=64)
+        weave(nc.vector.tensor_copy, 0, 0, 64)
+        weave(nc.scalar.copy, 0, 64, HALF)
+        weave(nc.vector.tensor_copy, 1, 0, 96)
+        weave(nc.scalar.copy, 1, 96, HALF)
         quantise_rr(0)
         nc.vector.quantize_mx(out=w2_c[:].bitcast(FP8X4), scales=w2_s[:], in_=w2_bf[:])
         quantise_rr(1)

@@ -17,10 +17,8 @@ ALU = mybir.AluOpType
 
 P = 128
 PACK = 4
-GROUP = 8
 RUN = 4
 HALF = V // 2
-BLOCKS = P // GROUP
 
 
 def tile_picked_yldpc_bp_p_kernel(tc, x_words, x_scales, w1, w2, damp, offs, pos1, pos2, pos3, out):
@@ -36,48 +34,44 @@ def tile_picked_yldpc_bp_p_kernel(tc, x_words, x_scales, w1, w2, damp, offs, pos
         xs = keep.tile([P, T], U8, name="xs", align_bytes=64)
         w1_raw = keep.tile([P, PACK, H], F32, name="w1_raw", align_bytes=64)
         w2_raw = keep.tile([P, PACK, N], F32, name="w2_raw", align_bytes=64)
-        damp_pad = keep.tile([P, PACK, 8], F32, name="damp_pad", align_bytes=64)
+        damp_t = keep.tile([P, PACK], F32, name="damp_t", align_bytes=64)
         warm = keep.tile([P, 8], F32, name="warm", align_bytes=64)
         warm_out = keep.tile([P, 8], F32, name="warm_out", align_bytes=64)
 
-        zero = lap.tile([P, 32], F32, name="zero", align_bytes=64, offset=3072 - 64)
         nc.vector.memset(xs[:].bitcast(I32), 0)
         nc.vector.memset(warm[:], 0.0)
-        nc.vector.memset(zero[:], 0.0)
         nc.sync.dma_start(xw[:].bitcast(I32), x_words[0].rearrange("p n t -> p (n t)").bitcast(I32))
         nc.sync.dma_start(offs_t[:], offs)
-        nc.sync.dma_start(pos_t[0][:], pos1)
         for q in range(4):
             nc.sync.dma_start(xs[32 * q : 32 * q + 4, :].bitcast(I32), x_scales[0, 4 * q : 4 * q + 4, :].bitcast(I32))
         nc.sync.dma_start(w1_raw[:], w1.rearrange("(p j) c -> p j c", j=PACK))
         nc.scalar.activation(warm_out[:], warm[:], ACT.Tanh, scale=0.5)
-        nc.sync.dma_start(pos_t[1][:], pos2)
-        nc.sync.dma_start(pos_t[2][:], pos3)
-        w2_rows = w2.rearrange("(b t r) n -> t b r n", t=PACK, r=GROUP)
-        for t in range(PACK):
-            nc.sync.dma_start(w2_raw[:, t, :], w2_rows[t])
-        damp_rows = damp.rearrange("(b t r) o -> t b r o", t=PACK, r=GROUP)
-        for t in range(PACK):
-            nc.sync.dma_start(damp_pad[:, t, 0:1], damp_rows[t])
+        nc.sync.dma_start(w2_raw[:], w2.rearrange("(p t) n -> p t n", t=PACK))
+        for d, pos in enumerate((pos1, pos2, pos3)):
+            nc.sync.dma_start(pos_t[d][:], pos)
+        nc.sync.dma_start(damp_t[:], damp.rearrange("(p t) o -> p (t o)", t=PACK))
 
         xg_s = keep.tile([P, S], U8, name="xg_s", align_bytes=64)
         xg_w = keep.tile([P, S], U32, name="xg_w", align_bytes=64)
         nc.vector.tensor_copy(xg_w[:], xw[:].indirect(offs_t[:]))
         nc.vector.tensor_copy(xg_s[:], xs[:].indirect(offs_t[:]))
 
-        w1_cols = w1_raw[:].rearrange("p j (b t u i) -> p t b u j i", t=PACK, u=GROUP // RUN, i=RUN)
-        w1_bf = [keep.tile([P, P * PACK], BF16, name="w1_bf%d" % t, align_bytes=64) for t in range(PACK - 1)]
-        w1_bf.append(w1_bf[0])
-        w1_c = [keep.tile([P, P], U32, name="w1_c%d" % t, align_bytes=64) for t in range(PACK)]
+        w1_cols = w1_raw[:].rearrange("p j (m u e) -> p u m j e", u=2, e=2)
+        w1_bf = [keep.tile([P, 2, P * PACK], BF16, name="w1_bf%d" % u, align_bytes=64) for u in range(2)]
+        w1_c = [keep.tile([P, P], U32, name="w1_c%d" % t, align_bytes=64) for t in range(PACK - 1)]
+        w1_c.append(lap.tile([P, P], U32, name="w1_c3", align_bytes=64, offset=0))
         w1_s = [keep.tile([P, P], U8, name="w1_s%d" % t, align_bytes=64) for t in range(PACK)]
         h = [keep.tile([P, S], F32, name="h%d" % t, align_bytes=64) for t in range(PACK)]
+        w2_bf = w1_bf[0][:, 0, :]
+        w2_c = keep.tile([P, N], U32, name="w2_c", align_bytes=64)
+        w2_s = keep.tile([P, N], U8, name="w2_s", align_bytes=64)
 
-        def cast_w1(copy, t, blocks):
-            dst = w1_bf[t][:].rearrange("p (b u i j) -> p b u j i", u=GROUP // RUN, i=RUN, j=PACK)
-            copy(dst[:, blocks], w1_cols[:, t, blocks])
+        def cast_w1(copy, u, rows):
+            dst = w1_bf[u][:].rearrange("p e (m j) -> p m j e", j=PACK)
+            copy(dst[:, rows], w1_cols[:, u, rows])
 
         def quantise_w1(t):
-            nc.vector.quantize_mx(out=w1_c[t][:].bitcast(FP8X4), scales=w1_s[t][:], in_=w1_bf[t][:])
+            nc.vector.quantize_mx(out=w1_c[t][:].bitcast(FP8X4), scales=w1_s[t][:], in_=w1_bf[t // 2][:, t % 2, :])
 
         def first_product(t, cols, name):
             pre = psum.tile([P, cols.stop - cols.start], F32, name=name, tag=name)
@@ -85,85 +79,79 @@ def tile_picked_yldpc_bp_p_kernel(tc, x_words, x_scales, w1, w2, damp, offs, pos
                                 rhs=xg_w[:, cols].bitcast(FP8X4), rhs_scale=xg_s[:, cols], start=True, stop=True)
             return pre
 
-        all_blocks = slice(0, BLOCKS)
-        cast_w1(nc.vector.tensor_copy, 0, slice(0, 10))
-        cast_w1(nc.scalar.copy, 0, slice(10, BLOCKS))
-        cast_w1(nc.scalar.copy, 2, all_blocks)
+        cast_w1(nc.vector.tensor_copy, 0, slice(0, 64))
+        cast_w1(nc.scalar.copy, 0, slice(64, P))
+        cast_w1(nc.vector.tensor_copy, 1, slice(0, 32))
+        cast_w1(nc.scalar.copy, 1, slice(64, P))
         quantise_w1(0)
-        cast_w1(nc.vector.tensor_copy, 1, all_blocks)
-        cast_w1(nc.vector.tensor_copy, 3, all_blocks)
-        for t in range(1, PACK):
-            quantise_w1(t)
+        cast_w1(nc.vector.tensor_copy, 1, slice(32, 64))
+        quantise_w1(1)
+        nc.vector.tensor_copy(w2_bf.rearrange("p (c i t) -> p c t i", i=RUN, t=PACK),
+                              w2_raw[:].rearrange("p t (c i) -> p c t i", i=RUN))
+        quantise_w1(2)
+        quantise_w1(3)
+        nc.vector.quantize_mx(out=w2_c[:].bitcast(FP8X4), scales=w2_s[:], in_=w2_bf)
         edges = [(0, 128, 256, 384, 512), (0, 256, 512), (0, 256, 512), (0, 256, 512)]
         parts = [(t, slice(a, b)) for t in range(PACK) for a, b in zip(edges[t], edges[t][1:])]
-        pres = [first_product(t, cols, "pre%d" % (k % 8)) for k, (t, cols) in enumerate(parts)]
+        banks = (0, 1, 2, 3, 4, 5, 6, 7, 0, 5)
+        pres = [first_product(t, cols, "pre%d" % bank) for bank, (t, cols) in zip(banks, parts)]
         for pre, (t, cols) in zip(pres, parts):
-            nc.scalar.activation(h[t][:, cols], pre[:], ACT.Tanh, scale=0.5, bias=zero[:, 0:1] if (t, cols.start) == (2, 0) else 0.0)
+            nc.scalar.activation(h[t][:, cols], pre[:], ACT.Tanh, scale=0.5)
 
-        w2_bf = keep.tile([P, N * PACK], BF16, name="w2_bf", align_bytes=64)
-        nc.scalar.copy(w2_bf[:].rearrange("p (c i t) -> p c t i", i=RUN, t=PACK),
-                       w2_raw[:].rearrange("p t (c i) -> p c t i", i=RUN))
-
-        halves = [slice(c * HALF, (c + 1) * HALF) for c in range(2)]
-        g1 = [lap.tile([P, V], F32, name="g1_%d" % t, align_bytes=64, offset=(0, 1024, 1024, 2048)[t]) for t in range(PACK)]
-        g2 = [lap.tile([P, V], F32, name="g2_%d" % t, align_bytes=64, offset=(3072, 2048, 4096, 5120)[t]) for t in range(PACK)]
-        z = [keep.tile([P, V], F32, name="z%d" % t, tag="z%d" % t, align_bytes=64) for t in range(PACK)]
-        lp = [keep.tile([P, V], F32, name="lp%d" % t, align_bytes=64) for t in range(PACK)]
-        lm = [lap.tile([P, V], F32, name="lm%d" % t, align_bytes=64, offset=(6144, 7168, 8192, 9728)[t]) for t in range(PACK)]
-        lmd = [keep.tile([P, V], F32, name="lmd%d" % t, align_bytes=64) for t in range(PACK)]
-        rr = keep.tile([P, PACK, V], BF16, name="rr", align_bytes=64)
-
-        def picked(d, t, cols):
-            return h[t][:].indirect(pos_t[d][:, cols.start // 16 : cols.stop // 16])
-
-        def logs(t, cols):
-            nc.scalar.activation(lm[t][:, cols], z[t][:, cols], ACT.Ln, scale=-0.98, bias=1.0)
-            nc.scalar.activation(lp[t][:, cols], z[t][:, cols], ACT.Ln, scale=0.98, bias=1.0)
-            nc.scalar.activation(lmd[t][:, cols], lm[t][:, cols], ACT.Copy, scale=damp_pad[:, t, 0:1])
-
-        def damped(t, cols):
-            nc.vector.scalar_tensor_tensor(rr[:, t, cols], lp[t][:, cols], damp_pad[:, t, 0:1], lmd[t][:, cols], ALU.mult, ALU.subtract)
-
-        whole = slice(0, V)
-
-        def first(t, cols):
-            nc.vector.tensor_copy(g1[t][:, cols], picked(0, t, cols))
-
-        def second(t, cols):
-            nc.vector.tensor_tensor(g2[t][:, cols], picked(1, t, cols), g1[t][:, cols], ALU.mult)
-
-        def third(t, cols):
-            nc.vector.tensor_tensor(z[t][:, cols], picked(2, t, cols), g2[t][:, cols], ALU.mult)
-
-        first(0, whole)
-        first(1, whole)
-        second(0, whole)
-        second(1, whole)
-        third(0, whole)
-        first(2, whole)
-        third(1, whole)
-        second(2, whole)
-        first(3, whole)
-        third(2, whole)
-        for step in (second, third):
-            for cols in halves:
-                step(3, cols)
-        logs(0, whole)
-        logs(1, whole)
-        logs(2, whole)
-        for cols in halves:
-            logs(3, cols)
-        for t in range(PACK - 1):
-            damped(t, whole)
-
-        woven = [lap.tile([P, HALF * PACK], BF16, name="woven%d" % c, align_bytes=64, offset=(10240, 11264)[c]) for c in range(2)]
+        g1 = [keep.tile([P, V], F32, name="g1_%d" % t, align_bytes=64) for t in range(PACK)]
+        g2 = [lap.tile([P, V], F32, name="g2_0", align_bytes=64, offset=0)]
+        g2.extend(keep.tile([P, V], F32, name="g2_%d" % t, align_bytes=64) for t in range(1, PACK))
+        z01 = keep.tile([P, 2, V], F32, name="z01", align_bytes=64)
+        z2 = keep.tile([P, V], F32, name="z2", align_bytes=64)
+        z3 = lap.tile([P, V], F32, name="z3", align_bytes=64, offset=1024)
+        z = [z01[:, 0, :], z01[:, 1, :], z2[:], z3[:]]
+        diff = keep.tile([P, 2, PACK, HALF], F32, name="diff", align_bytes=64)
+        woven = [lap.tile([P, HALF * PACK], BF16, name="woven0", align_bytes=64, offset=1024),
+                 keep.tile([P, HALF * PACK], BF16, name="woven1", align_bytes=64)]
         rr_c = [keep.tile([P, HALF], U32, name="rr_c%d" % c, align_bytes=64) for c in range(2)]
         rr_s = [keep.tile([P, HALF], U8, name="rr_s%d" % c, align_bytes=64) for c in range(2)]
         res = [keep.tile([P, HALF], F32, name="res%d" % c, align_bytes=64) for c in range(2)]
 
-        def weave(copy, c, a, b):
-            copy(woven[c][:, PACK * a : PACK * b].rearrange("p (c i t) -> p c t i", i=RUN, t=PACK),
-                 rr[:, :, c * HALF + a : c * HALF + b].rearrange("p t (c i) -> p c t i", i=RUN))
+        def picked(d, t):
+            return h[t][:].indirect(pos_t[d][:])
+
+        def first_on_vector(t):
+            nc.vector.tensor_copy(g1[t][:], picked(0, t))
+
+        def first_on_scalar(t):
+            nc.scalar.activation(g1[t][:], picked(0, t), ACT.Copy)
+
+        def second(t):
+            nc.vector.tensor_tensor(g2[t][:], picked(1, t), g1[t][:], ALU.mult)
+
+        def third(t):
+            nc.vector.tensor_tensor(z[t], picked(2, t), g2[t][:], ALU.mult)
+
+        for pair, first in enumerate((first_on_vector, first_on_scalar)):
+            for step in (first, second, third):
+                for t in (2 * pair, 2 * pair + 1):
+                    step(t)
+
+        pieces = [
+            (z01[:].rearrange("p t (c v) -> p t c v", c=2), diff[:, :, 0:2, :].rearrange("p c t v -> p t c v")),
+            (z2[:].rearrange("p (c v) -> p c v", c=2), diff[:, :, 2, :]),
+            (z3[:, 0:HALF], diff[:, 0, 3, :]),
+            (z3[:, HALF:V], diff[:, 1, 3, :]),
+        ]
+        logs = []
+        for k, (src, dst) in enumerate(pieces):
+            lm = keep.tile(list(src.shape), F32, name="lm%d" % k, align_bytes=64)
+            lp = keep.tile(list(src.shape), F32, name="lp%d" % k, align_bytes=64)
+            nc.scalar.activation(lm[:], src, ACT.Ln, scale=-0.98, bias=1.0)
+            nc.scalar.activation(lp[:], src, ACT.Ln, scale=0.98, bias=1.0)
+            logs.append((lp, lm))
+        for (lp, lm), (src, dst) in zip(logs, pieces):
+            nc.vector.tensor_tensor(dst, lp[:], lm[:], ALU.subtract)
+
+        factor = damp_t[:].unsqueeze(2).unsqueeze(1).to_broadcast([P, HALF // RUN, PACK, RUN])
+        for c in range(2):
+            nc.vector.tensor_tensor(woven[c][:].rearrange("p (c i t) -> p c t i", i=RUN, t=PACK),
+                                    diff[:, c].rearrange("p t (c i) -> p c t i", i=RUN), factor, ALU.mult)
 
         def quantise_rr(c):
             nc.vector.quantize_mx(out=rr_c[c][:].bitcast(FP8X4), scales=rr_s[c][:], in_=woven[c][:])
@@ -173,18 +161,9 @@ def tile_picked_yldpc_bp_p_kernel(tc, x_words, x_scales, w1, w2, damp, offs, pos
             nc.tensor.matmul_mx(out=acc[:], lhsT=w2_c[:].bitcast(FP8X4), lhsT_scale=w2_s[:],
                                 rhs=rr_c[c][:].bitcast(FP8X4), rhs_scale=rr_s[c][:], start=True, stop=True)
             copy(res[c][:], acc[:])
-            nc.sync.dma_start(out[:, halves[c]], res[c][:])
+            nc.sync.dma_start(out[:, c * HALF : (c + 1) * HALF], res[c][:])
 
-        for cols in halves:
-            damped(PACK - 1, cols)
-        w2_c = lap.tile([P, N], U32, name="w2_c", align_bytes=64, offset=9728)
-        w2_s = keep.tile([P, N], U8, name="w2_s", align_bytes=64)
-        weave(nc.vector.tensor_copy, 0, 0, 64)
-        weave(nc.scalar.copy, 0, 64, HALF)
-        weave(nc.vector.tensor_copy, 1, 0, 96)
-        weave(nc.scalar.copy, 1, 96, HALF)
-        quantise_rr(0)
-        nc.vector.quantize_mx(out=w2_c[:].bitcast(FP8X4), scales=w2_s[:], in_=w2_bf[:])
-        quantise_rr(1)
+        for c in range(2):
+            quantise_rr(c)
         second_product(nc.scalar.copy, 0)
         second_product(nc.vector.tensor_copy, 1)

@@ -17,6 +17,8 @@ ALU = mybir.AluOpType
 
 P = 128
 PACK = 4
+GROUP = 8
+BLOCKS = P // GROUP
 RUN = 4
 HALF = V // 2
 
@@ -34,6 +36,7 @@ def tile_picked_yldpc_bp_p_kernel(tc, x_words, x_scales, w1, w2, damp, offs, pos
         xs = keep.tile([P, T], U8, name="xs", align_bytes=64)
         w1_raw = keep.tile([P, PACK, H], F32, name="w1_raw", align_bytes=64)
         w2_raw = keep.tile([P, PACK, N], F32, name="w2_raw", align_bytes=64)
+        damp_pad = keep.tile([P, 2, 8], F32, name="damp_pad", align_bytes=64)
         damp_t = keep.tile([P, PACK], F32, name="damp_t", align_bytes=64)
         warm = keep.tile([P, 8], F32, name="warm", align_bytes=64)
         warm_out = keep.tile([P, 8], F32, name="warm_out", align_bytes=64)
@@ -46,50 +49,62 @@ def tile_picked_yldpc_bp_p_kernel(tc, x_words, x_scales, w1, w2, damp, offs, pos
             nc.sync.dma_start(xs[32 * q : 32 * q + 4, :].bitcast(I32), x_scales[0, 4 * q : 4 * q + 4, :].bitcast(I32))
         nc.sync.dma_start(w1_raw[:], w1.rearrange("(p j) c -> p j c", j=PACK))
         nc.scalar.activation(warm_out[:], warm[:], ACT.Tanh, scale=0.5)
-        nc.sync.dma_start(w2_raw[:], w2.rearrange("(p t) n -> p t n", t=PACK))
+        w2_rows = w2.rearrange("(b u r e) n -> u b r (e n)", u=2, r=GROUP, e=2)
+        for u in range(2):
+            nc.sync.dma_start(w2_raw[:, 2 * u : 2 * u + 2, :].rearrange("p e n -> p (e n)"), w2_rows[u])
         for d, pos in enumerate((pos1, pos2, pos3)):
             nc.sync.dma_start(pos_t[d][:], pos)
-        nc.sync.dma_start(damp_t[:], damp.rearrange("(p t) o -> p (t o)", t=PACK))
+        damp_rows = damp.rearrange("(b u r e) o -> u b r (e o)", u=2, r=GROUP, e=2)
+        for u in range(2):
+            nc.sync.dma_start(damp_pad[:, u, 0:2], damp_rows[u])
+        nc.gpsimd.tensor_copy(damp_t[:].rearrange("p (u e) -> p u e", u=2), damp_pad[:, :, 0:2])
 
         xg_s = keep.tile([P, S], U8, name="xg_s", align_bytes=64)
         xg_w = keep.tile([P, S], U32, name="xg_w", align_bytes=64)
         nc.vector.tensor_copy(xg_w[:], xw[:].indirect(offs_t[:]))
         nc.vector.tensor_copy(xg_s[:], xs[:].indirect(offs_t[:]))
 
-        w1_cols = w1_raw[:].rearrange("p j (m u e) -> p u m j e", u=2, e=2)
+        w1_cols = w1_raw[:].rearrange("p j (b u h i e) -> p u b h j i e", u=2, h=4, i=2, e=2)
         w1_bf = [keep.tile([P, 2, P * PACK], BF16, name="w1_bf%d" % u, align_bytes=64) for u in range(2)]
-        w1_c = [keep.tile([P, P], U32, name="w1_c%d" % t, align_bytes=64) for t in range(PACK - 1)]
-        w1_c.append(lap.tile([P, P], U32, name="w1_c3", align_bytes=64, offset=0))
-        w1_s = [keep.tile([P, P], U8, name="w1_s%d" % t, align_bytes=64) for t in range(PACK)]
+        c_early = [keep.tile([P, P], U32, name="w1_c%d" % t, align_bytes=64) for t in range(2)]
+        s_early = [keep.tile([P, P], U8, name="w1_s%d" % t, align_bytes=64) for t in range(2)]
+        c_late = lap.tile([P, 2 * P], U32, name="w1_c23", align_bytes=64, offset=0)
+        s_late = keep.tile([P, 2 * P], U8, name="w1_s23", align_bytes=64)
+        w1_c = [c_early[0][:], c_early[1][:], c_late[:, 0:P], c_late[:, P : 2 * P]]
+        w1_s = [s_early[0][:], s_early[1][:], s_late[:, 0:P], s_late[:, P : 2 * P]]
         h = [keep.tile([P, S], F32, name="h%d" % t, align_bytes=64) for t in range(PACK)]
         w2_bf = w1_bf[0][:, 0, :]
         w2_c = keep.tile([P, N], U32, name="w2_c", align_bytes=64)
         w2_s = keep.tile([P, N], U8, name="w2_s", align_bytes=64)
 
-        def cast_w1(copy, u, rows):
-            dst = w1_bf[u][:].rearrange("p e (m j) -> p m j e", j=PACK)
-            copy(dst[:, rows], w1_cols[:, u, rows])
+        def staged(u):
+            return w1_bf[u][:].rearrange("p e (b h i j) -> p b h j i e", h=4, i=2, j=PACK)
+
+        def cast_slot(copy, e, blocks):
+            copy(staged(0)[:, blocks, :, :, :, e], w1_cols[:, 0, blocks, :, :, :, e])
+
+        def cast_pair(copy, blocks):
+            copy(staged(1)[:, blocks], w1_cols[:, 1, blocks])
 
         def quantise_w1(t):
-            nc.vector.quantize_mx(out=w1_c[t][:].bitcast(FP8X4), scales=w1_s[t][:], in_=w1_bf[t // 2][:, t % 2, :])
+            nc.vector.quantize_mx(out=w1_c[t].bitcast(FP8X4), scales=w1_s[t], in_=w1_bf[0][:, t, :])
 
         def first_product(t, cols, name):
             pre = psum.tile([P, cols.stop - cols.start], F32, name=name, tag=name)
-            nc.tensor.matmul_mx(out=pre[:], lhsT=w1_c[t][:].bitcast(FP8X4), lhsT_scale=w1_s[t][:],
+            nc.tensor.matmul_mx(out=pre[:], lhsT=w1_c[t].bitcast(FP8X4), lhsT_scale=w1_s[t],
                                 rhs=xg_w[:, cols].bitcast(FP8X4), rhs_scale=xg_s[:, cols], start=True, stop=True)
             return pre
 
-        cast_w1(nc.vector.tensor_copy, 0, slice(0, 64))
-        cast_w1(nc.scalar.copy, 0, slice(64, P))
-        cast_w1(nc.vector.tensor_copy, 1, slice(0, 32))
-        cast_w1(nc.scalar.copy, 1, slice(64, P))
+        cast_slot(nc.vector.tensor_copy, 0, slice(0, 8))
+        cast_slot(nc.scalar.copy, 0, slice(8, BLOCKS))
+        cast_pair(nc.scalar.copy, slice(4, BLOCKS))
+        cast_slot(nc.vector.tensor_copy, 1, slice(0, BLOCKS))
         quantise_w1(0)
-        cast_w1(nc.vector.tensor_copy, 1, slice(32, 64))
+        cast_pair(nc.vector.tensor_copy, slice(0, 4))
         quantise_w1(1)
         nc.vector.tensor_copy(w2_bf.rearrange("p (c i t) -> p c t i", i=RUN, t=PACK),
                               w2_raw[:].rearrange("p t (c i) -> p c t i", i=RUN))
-        quantise_w1(2)
-        quantise_w1(3)
+        nc.vector.quantize_mx(out=c_late[:].bitcast(FP8X4), scales=s_late[:], in_=w1_bf[1][:].rearrange("p e c -> p (e c)"))
         nc.vector.quantize_mx(out=w2_c[:].bitcast(FP8X4), scales=w2_s[:], in_=w2_bf)
         edges = [(0, 128, 256, 384, 512), (0, 256, 512), (0, 256, 512), (0, 256, 512)]
         parts = [(t, slice(a, b)) for t in range(PACK) for a, b in zip(edges[t], edges[t][1:])]
@@ -132,6 +147,7 @@ def tile_picked_yldpc_bp_p_kernel(tc, x_words, x_scales, w1, w2, damp, offs, pos
                 for t in (2 * pair, 2 * pair + 1):
                     step(t)
 
+
         pieces = [
             (z01[:].rearrange("p t (c v) -> p t c v", c=2), diff[:, :, 0:2, :].rearrange("p c t v -> p t c v")),
             (z2[:].rearrange("p (c v) -> p c v", c=2), diff[:, :, 2, :]),
@@ -148,10 +164,17 @@ def tile_picked_yldpc_bp_p_kernel(tc, x_words, x_scales, w1, w2, damp, offs, pos
         for (lp, lm), (src, dst) in zip(logs, pieces):
             nc.vector.tensor_tensor(dst, lp[:], lm[:], ALU.subtract)
 
+
         factor = damp_t[:].unsqueeze(2).unsqueeze(1).to_broadcast([P, HALF // RUN, PACK, RUN])
-        for c in range(2):
-            nc.vector.tensor_tensor(woven[c][:].rearrange("p (c i t) -> p c t i", i=RUN, t=PACK),
-                                    diff[:, c].rearrange("p t (c i) -> p c t i", i=RUN), factor, ALU.mult)
+        nc.vector.tensor_tensor(woven[0][:].rearrange("p (c i t) -> p c t i", i=RUN, t=PACK),
+                                diff[:, 0].rearrange("p t (c i) -> p c t i", i=RUN), factor, ALU.mult)
+        rr_late = keep.tile([P, PACK, HALF], BF16, name="rr_late", align_bytes=64)
+        for t in range(PACK):
+            nc.scalar.activation(rr_late[:, t, :], diff[:, 1, t, :], ACT.Copy, scale=damp_t[:, t : t + 1])
+        for copy, a, b in ((nc.vector.tensor_copy, 0, 96), (nc.scalar.copy, 96, HALF)):
+            copy(woven[1][:, PACK * a : PACK * b].rearrange("p (c i t) -> p c t i", i=RUN, t=PACK),
+                 rr_late[:, :, a:b].rearrange("p t (c i) -> p c t i", i=RUN))
+
 
         def quantise_rr(c):
             nc.vector.quantize_mx(out=rr_c[c][:].bitcast(FP8X4), scales=rr_s[c][:], in_=woven[c][:])

@@ -21,13 +21,14 @@ GROUP = 8
 BLOCKS = P // GROUP
 RUN = 4
 HALF = V // 2
+APART = 16384
 
 
 def tile_picked_yldpc_bp_p_kernel(tc, x_words, x_scales, w1, w2, damp, offs, pos1, pos2, pos3, out):
     nc = tc.nc
     with ExitStack() as ctx:
         keep = ctx.enter_context(tc.tile_pool(name="keep", bufs=1))
-        lap = ctx.enter_context(tc.tile_pool(name="lap", bufs=1))
+        far = ctx.enter_context(tc.tile_pool(name="far", bufs=1))
         psum = ctx.enter_context(tc.psum_pool(name="psum", bufs=1))
 
         offs_t = keep.tile([P, S // 16], U16, name="offs_t")
@@ -68,11 +69,11 @@ def tile_picked_yldpc_bp_p_kernel(tc, x_words, x_scales, w1, w2, damp, offs, pos
         w1_bf = [keep.tile([P, 2, P * PACK], BF16, name="w1_bf%d" % u, align_bytes=64) for u in range(2)]
         c_early = [keep.tile([P, P], U32, name="w1_c%d" % t, align_bytes=64) for t in range(2)]
         s_early = [keep.tile([P, P], U8, name="w1_s%d" % t, align_bytes=64) for t in range(2)]
-        c_late = lap.tile([P, 2 * P], U32, name="w1_c23", align_bytes=64, offset=0)
+        c_late = far.tile([P, 2 * P], U32, name="w1_c23", align_bytes=64, offset=5 * APART + 128)
         s_late = keep.tile([P, 2 * P], U8, name="w1_s23", align_bytes=64)
         w1_c = [c_early[0][:], c_early[1][:], c_late[:, 0:P], c_late[:, P : 2 * P]]
         w1_s = [s_early[0][:], s_early[1][:], s_late[:, 0:P], s_late[:, P : 2 * P]]
-        h = [keep.tile([P, S], F32, name="h%d" % t, align_bytes=64) for t in range(PACK)]
+        h = [far.tile([P, S], F32, name="h%d" % t, align_bytes=256, offset=t * APART) for t in range(PACK)]
         w2_bf = w1_bf[0][:, 0, :]
         w2_c = keep.tile([P, N], U32, name="w2_c", align_bytes=64)
         w2_s = keep.tile([P, N], U8, name="w2_s", align_bytes=64)
@@ -113,15 +114,14 @@ def tile_picked_yldpc_bp_p_kernel(tc, x_words, x_scales, w1, w2, damp, offs, pos
         for pre, (t, cols) in zip(pres, parts):
             nc.scalar.activation(h[t][:, cols], pre[:], ACT.Tanh, scale=0.5)
 
-        g1 = [keep.tile([P, V], F32, name="g1_%d" % t, align_bytes=64) for t in range(PACK)]
-        g2 = [lap.tile([P, V], F32, name="g2_0", align_bytes=64, offset=0)]
-        g2.extend(keep.tile([P, V], F32, name="g2_%d" % t, align_bytes=64) for t in range(1, PACK))
-        z01 = keep.tile([P, 2, V], F32, name="z01", align_bytes=64)
-        z2 = keep.tile([P, V], F32, name="z2", align_bytes=64)
-        z3 = lap.tile([P, V], F32, name="z3", align_bytes=64, offset=1024)
+        g1 = [far.tile([P, V], F32, name="g1_%d" % t, align_bytes=64, offset=4 * APART + t * 2048 + 64) for t in range(PACK)]
+        g2 = [far.tile([P, V], F32, name="g2_%d" % t, align_bytes=64, offset=5 * APART + t * 2048 + 128) for t in range(PACK)]
+        z01 = far.tile([P, 2, V], F32, name="z01", align_bytes=64, offset=6 * APART + 192)
+        z2 = far.tile([P, V], F32, name="z2", align_bytes=64, offset=6 * APART + 4096 + 192)
+        z3 = far.tile([P, V], F32, name="z3", align_bytes=64, offset=6 * APART + 6144 + 192)
         z = [z01[:, 0, :], z01[:, 1, :], z2[:], z3[:]]
-        diff = keep.tile([P, 2, PACK, HALF], F32, name="diff", align_bytes=64)
-        woven = [lap.tile([P, HALF * PACK], BF16, name="woven0", align_bytes=64, offset=1024),
+        diff = far.tile([P, 2, PACK, HALF], F32, name="diff", align_bytes=64, offset=9 * APART + 128)
+        woven = [far.tile([P, HALF * PACK], BF16, name="woven0", align_bytes=64, offset=6 * APART + 6144 + 192),
                  keep.tile([P, HALF * PACK], BF16, name="woven1", align_bytes=64)]
         rr_c = [keep.tile([P, HALF], U32, name="rr_c%d" % c, align_bytes=64) for c in range(2)]
         rr_s = [keep.tile([P, HALF], U8, name="rr_s%d" % c, align_bytes=64) for c in range(2)]
@@ -156,8 +156,8 @@ def tile_picked_yldpc_bp_p_kernel(tc, x_words, x_scales, w1, w2, damp, offs, pos
         ]
         logs = []
         for k, (src, dst) in enumerate(pieces):
-            lm = keep.tile(list(src.shape), F32, name="lm%d" % k, align_bytes=64)
-            lp = keep.tile(list(src.shape), F32, name="lp%d" % k, align_bytes=64)
+            lm = far.tile(list(src.shape), F32, name="lm%d" % k, align_bytes=64, offset=7 * APART + k * 4096)
+            lp = far.tile(list(src.shape), F32, name="lp%d" % k, align_bytes=64, offset=8 * APART + k * 4096 + 64)
             nc.scalar.activation(lm[:], src, ACT.Ln, scale=-0.98, bias=1.0)
             nc.scalar.activation(lp[:], src, ACT.Ln, scale=0.98, bias=1.0)
             logs.append((lp, lm))

from contextlib import ExitStack

import concourse.mybir as mybir

K, T, S, V, H, N = 512, 1024, 512, 256, 512, 128
FLOPS = 2 * K * H * S + 2 * H * N * V

F32 = mybir.dt.float32
BF16 = mybir.dt.bfloat16
I32 = mybir.dt.int32
U32 = mybir.dt.uint32
U16 = mybir.dt.uint16
U8 = mybir.dt.uint8
FP8X4 = mybir.dt.float8_e4m3fn_x4
ACT = mybir.ActivationFunctionType
ALU = mybir.AluOpType

P = 128
PACK = 4
GROUP = 8
BLOCKS = P // GROUP
RUN = 4
HALF = V // 2
APART = 16384


def tile_picked_yldpc_bp_p_kernel(tc, x_words, x_scales, w1, w2, damp, offs, pos1, pos2, pos3, out):
    nc = tc.nc
    with ExitStack() as ctx:
        keep = ctx.enter_context(tc.tile_pool(name="keep", bufs=1))
        far = ctx.enter_context(tc.tile_pool(name="far", bufs=1))
        psum = ctx.enter_context(tc.psum_pool(name="psum", bufs=1))

        offs_t = keep.tile([P, S // 16], U16, name="offs_t")
        pos_t = [keep.tile([P, V // 16], U16, name="pos_t%d" % d) for d in range(3)]
        xw = keep.tile([P, T], U32, name="xw", align_bytes=64)
        xs = keep.tile([P, T], U8, name="xs", align_bytes=64)
        w1_raw = keep.tile([P, PACK, H], F32, name="w1_raw", align_bytes=64)
        w2_raw = keep.tile([P, PACK, N], F32, name="w2_raw", align_bytes=64)
        damp_pad = keep.tile([P, 2, 8], F32, name="damp_pad", align_bytes=64)
        damp_t = keep.tile([P, PACK], F32, name="damp_t", align_bytes=64)
        warm = keep.tile([P, 8], F32, name="warm", align_bytes=64)
        warm_out = keep.tile([P, 8], F32, name="warm_out", align_bytes=64)

        nc.vector.memset(xs[:].bitcast(I32), 0)
        nc.vector.memset(warm[:], 0.0)
        nc.sync.dma_start(xw[:].bitcast(I32), x_words[0].rearrange("p n t -> p (n t)").bitcast(I32))
        nc.sync.dma_start(offs_t[:], offs)
        for q in range(4):
            nc.sync.dma_start(xs[32 * q : 32 * q + 4, :].bitcast(I32), x_scales[0, 4 * q : 4 * q + 4, :].bitcast(I32))
        nc.sync.dma_start(w1_raw[:], w1.rearrange("(p j) c -> p j c", j=PACK))
        nc.scalar.activation(warm_out[:], warm[:], ACT.Tanh, scale=0.5)
        w2_rows = w2.rearrange("(b u r e) n -> u b r (e n)", u=2, r=GROUP, e=2)
        for u in range(2):
            nc.sync.dma_start(w2_raw[:, 2 * u : 2 * u + 2, :].rearrange("p e n -> p (e n)"), w2_rows[u])
        for d, pos in enumerate((pos1, pos2, pos3)):
            nc.sync.dma_start(pos_t[d][:], pos)
        damp_rows = damp.rearrange("(b u r e) o -> u b r (e o)", u=2, r=GROUP, e=2)
        for u in range(2):
            nc.sync.dma_start(damp_pad[:, u, 0:2], damp_rows[u])
        nc.gpsimd.tensor_copy(damp_t[:].rearrange("p (u e) -> p u e", u=2), damp_pad[:, :, 0:2])

        xg_s = keep.tile([P, S], U8, name="xg_s", align_bytes=64)
        xg_w = keep.tile([P, S], U32, name="xg_w", align_bytes=64)
        nc.vector.tensor_copy(xg_w[:], xw[:].indirect(offs_t[:]))
        nc.vector.tensor_copy(xg_s[:], xs[:].indirect(offs_t[:]))

        w1_cols = w1_raw[:].rearrange("p j (b u h i e) -> p u b h j i e", u=2, h=4, i=2, e=2)
        w1_bf = [keep.tile([P, 2, P * PACK], BF16, name="w1_bf%d" % u, align_bytes=64) for u in range(2)]
        c_early = [keep.tile([P, P], U32, name="w1_c%d" % t, align_bytes=64) for t in range(2)]
        s_early = [keep.tile([P, P], U8, name="w1_s%d" % t, align_bytes=64) for t in range(2)]
        c_late = far.tile([P, 2 * P], U32, name="w1_c23", align_bytes=64, offset=5 * APART + 128)
        s_late = keep.tile([P, 2 * P], U8, name="w1_s23", align_bytes=64)
        w1_c = [c_early[0][:], c_early[1][:], c_late[:, 0:P], c_late[:, P : 2 * P]]
        w1_s = [s_early[0][:], s_early[1][:], s_late[:, 0:P], s_late[:, P : 2 * P]]
        h = [far.tile([P, S], F32, name="h%d" % t, align_bytes=256, offset=t * APART) for t in range(PACK)]
        w2_bf = w1_bf[0][:, 0, :]
        w2_c = keep.tile([P, N], U32, name="w2_c", align_bytes=64)
        w2_s = keep.tile([P, N], U8, name="w2_s", align_bytes=64)

        def staged(u):
            return w1_bf[u][:].rearrange("p e (b h i j) -> p b h j i e", h=4, i=2, j=PACK)

        def cast_slot(copy, e, blocks):
            copy(staged(0)[:, blocks, :, :, :, e], w1_cols[:, 0, blocks, :, :, :, e])

        def cast_pair(copy, blocks):
            copy(staged(1)[:, blocks], w1_cols[:, 1, blocks])

        def quantise_w1(t):
            nc.vector.quantize_mx(out=w1_c[t].bitcast(FP8X4), scales=w1_s[t], in_=w1_bf[0][:, t, :])

        def first_product(t, cols, name):
            pre = psum.tile([P, cols.stop - cols.start], F32, name=name, tag=name)
            nc.tensor.matmul_mx(out=pre[:], lhsT=w1_c[t].bitcast(FP8X4), lhsT_scale=w1_s[t],
                                rhs=xg_w[:, cols].bitcast(FP8X4), rhs_scale=xg_s[:, cols], start=True, stop=True)
            return pre

        cast_slot(nc.vector.tensor_copy, 0, slice(0, 8))
        cast_slot(nc.scalar.copy, 0, slice(8, BLOCKS))
        cast_pair(nc.scalar.copy, slice(4, BLOCKS))
        cast_slot(nc.vector.tensor_copy, 1, slice(0, BLOCKS))
        quantise_w1(0)
        cast_pair(nc.vector.tensor_copy, slice(0, 4))
        quantise_w1(1)
        nc.vector.tensor_copy(w2_bf.rearrange("p (c i t) -> p c t i", i=RUN, t=PACK),
                              w2_raw[:].rearrange("p t (c i) -> p c t i", i=RUN))
        nc.vector.quantize_mx(out=c_late[:].bitcast(FP8X4), scales=s_late[:], in_=w1_bf[1][:].rearrange("p e c -> p (e c)"))
        nc.vector.quantize_mx(out=w2_c[:].bitcast(FP8X4), scales=w2_s[:], in_=w2_bf)
        edges = [(0, 128, 256, 384, 512), (0, 256, 512), (0, 256, 512), (0, 256, 512)]
        parts = [(t, slice(a, b)) for t in range(PACK) for a, b in zip(edges[t], edges[t][1:])]
        banks = (0, 1, 2, 3, 4, 5, 6, 7, 0, 5)
        pres = [first_product(t, cols, "pre%d" % bank) for bank, (t, cols) in zip(banks, parts)]
        for pre, (t, cols) in zip(pres, parts):
            nc.scalar.activation(h[t][:, cols], pre[:], ACT.Tanh, scale=0.5)

        g1 = [far.tile([P, V], F32, name="g1_%d" % t, align_bytes=64, offset=4 * APART + t * 2048 + 64) for t in range(PACK)]
        g2 = [far.tile([P, V], F32, name="g2_%d" % t, align_bytes=64, offset=5 * APART + t * 2048 + 128) for t in range(PACK)]
        z01 = far.tile([P, 2, V], F32, name="z01", align_bytes=64, offset=6 * APART + 192)
        z2 = far.tile([P, V], F32, name="z2", align_bytes=64, offset=6 * APART + 4096 + 192)
        z3 = far.tile([P, V], F32, name="z3", align_bytes=64, offset=6 * APART + 6144 + 192)
        z = [z01[:, 0, :], z01[:, 1, :], z2[:], z3[:]]
        diff = far.tile([P, 2, PACK, HALF], F32, name="diff", align_bytes=64, offset=9 * APART + 128)
        woven = [far.tile([P, HALF * PACK], BF16, name="woven0", align_bytes=64, offset=6 * APART + 6144 + 192),
                 keep.tile([P, HALF * PACK], BF16, name="woven1", align_bytes=64)]
        rr_c = [keep.tile([P, HALF], U32, name="rr_c%d" % c, align_bytes=64) for c in range(2)]
        rr_s = [keep.tile([P, HALF], U8, name="rr_s%d" % c, align_bytes=64) for c in range(2)]
        res = [keep.tile([P, HALF], F32, name="res%d" % c, align_bytes=64) for c in range(2)]

        def picked(d, t):
            return h[t][:].indirect(pos_t[d][:])

        def first_on_vector(t):
            nc.vector.tensor_copy(g1[t][:], picked(0, t))

        def first_on_scalar(t):
            nc.scalar.activation(g1[t][:], picked(0, t), ACT.Copy)

        def second(t):
            nc.vector.tensor_tensor(g2[t][:], picked(1, t), g1[t][:], ALU.mult)

        def third(t):
            nc.vector.tensor_tensor(z[t], picked(2, t), g2[t][:], ALU.mult)

        for pair, first in enumerate((first_on_vector, first_on_scalar)):
            for step in (first, second, third):
                for t in (2 * pair, 2 * pair + 1):
                    step(t)


        pieces = [
            (z01[:].rearrange("p t (c v) -> p t c v", c=2), diff[:, :, 0:2, :].rearrange("p c t v -> p t c v")),
            (z2[:].rearrange("p (c v) -> p c v", c=2), diff[:, :, 2, :]),
            (z3[:, 0:HALF], diff[:, 0, 3, :]),
            (z3[:, HALF:V], diff[:, 1, 3, :]),
        ]
        logs = []
        for k, (src, dst) in enumerate(pieces):
            lm = far.tile(list(src.shape), F32, name="lm%d" % k, align_bytes=64, offset=7 * APART + k * 4096)
            lp = far.tile(list(src.shape), F32, name="lp%d" % k, align_bytes=64, offset=8 * APART + k * 4096 + 64)
            nc.scalar.activation(lm[:], src, ACT.Ln, scale=-0.98, bias=1.0)
            nc.scalar.activation(lp[:], src, ACT.Ln, scale=0.98, bias=1.0)
            logs.append((lp, lm))
        for (lp, lm), (src, dst) in zip(logs, pieces):
            nc.vector.tensor_tensor(dst, lp[:], lm[:], ALU.subtract)


        factor = damp_t[:].unsqueeze(2).unsqueeze(1).to_broadcast([P, HALF // RUN, PACK, RUN])
        nc.vector.tensor_tensor(woven[0][:].rearrange("p (c i t) -> p c t i", i=RUN, t=PACK),
                                diff[:, 0].rearrange("p t (c i) -> p c t i", i=RUN), factor, ALU.mult)
        rr_late = keep.tile([P, PACK, HALF], BF16, name="rr_late", align_bytes=64)
        for t in range(PACK):
            nc.scalar.activation(rr_late[:, t, :], diff[:, 1, t, :], ACT.Copy, scale=damp_t[:, t : t + 1])
        for copy, a, b in ((nc.vector.tensor_copy, 0, 96), (nc.scalar.copy, 96, HALF)):
            copy(woven[1][:, PACK * a : PACK * b].rearrange("p (c i t) -> p c t i", i=RUN, t=PACK),
                 rr_late[:, :, a:b].rearrange("p t (c i) -> p c t i", i=RUN))


        def quantise_rr(c):
            nc.vector.quantize_mx(out=rr_c[c][:].bitcast(FP8X4), scales=rr_s[c][:], in_=woven[c][:])

        def second_product(copy, c):
            acc = psum.tile([P, HALF], F32, name="acc%d" % c, tag="pre%d" % (c + 2))
            nc.tensor.matmul_mx(out=acc[:], lhsT=w2_c[:].bitcast(FP8X4), lhsT_scale=w2_s[:],
                                rhs=rr_c[c][:].bitcast(FP8X4), rhs_scale=rr_s[c][:], start=True, stop=True)
            copy(res[c][:], acc[:])
            nc.sync.dma_start(out[:, c * HALF : (c + 1) * HALF], res[c][:])

        for c in range(2):
            quantise_rr(c)
        second_product(nc.scalar.copy, 0)
        second_product(nc.vector.tensor_copy, 1)
